import numpy as np
import ml_dtypes


def mxq(x, axis, fmt="e4m3"):
    dtype, down = {"e4m3": (ml_dtypes.float8_e4m3fn, 7), "e5m2": (ml_dtypes.float8_e5m2, 14)}[fmt]
    v = np.moveaxis(np.asarray(x, np.float32).astype(ml_dtypes.bfloat16).astype(np.float64), axis, -1)
    blocks = v.reshape(v.shape[:-1] + (-1, 32))
    amax = np.abs(blocks).max(-1, keepdims=True)
    byte = np.maximum(np.where(amax > 0, np.frexp(amax)[1] - 1 + 127, 0) - down, 1)
    scale = np.exp2(byte - 127.0)
    codes = (blocks / scale).astype(np.float32).astype(dtype).astype(np.float64)
    return np.moveaxis((codes * scale).reshape(v.shape), -1, axis)


WIDE = False


def mx_kscale(k):
    if not WIDE:
        return np.ones(k)
    levels = np.array([10, -10, 5, -5, 0])
    if k % 512:
        return np.exp2(np.random.permutation(np.resize(levels, k // 32))).repeat(32)
    a = np.empty((k // 512, 16))
    for p in range(k // 512):
        a[p, :8] = np.random.permutation(np.resize(levels, 8))
        for g in range(8):
            far = levels[np.abs(levels - a[p, g]) >= 10]
            a[p, g + 8] = far[np.random.randint(len(far))]
    return np.exp2(a.ravel()).repeat(32)


def f64(x):
    return np.asarray(x).astype(np.float64)


def striped(idx):
    return np.tile(idx.reshape(-1, 16).T, (8, 1)).astype(np.uint16)


def unstriped(offs):
    return offs[:16].T.reshape(-1).astype(np.int64)


E2M1 = np.array([0.0, 0.5, 1.0, 1.5, 2.0, 3.0, 4.0, 6.0, -0.0, -0.5, -1.0, -1.5, -2.0, -3.0, -4.0, -6.0])


def pack_weight(w, fmt):
    k, n = w.shape
    w = f64(np.asarray(w, np.float32).astype(ml_dtypes.bfloat16)).reshape(k // 32, 32, n)
    amax = np.abs(w).max(1)
    if fmt == "e4m3":
        byte = np.frexp(amax)[1] - 1 + 127 - 7
    else:
        mant, ex = np.frexp(amax / 6.0)
        byte = np.where(mant > 0.5, ex, ex - 1) + 127
    byte = np.clip(np.where(amax > 0, byte, 1), 1, 254)
    scaled = (w * np.exp2(127.0 - byte)[:, None, :]).reshape(k, n).astype(np.float32)
    by_word = np.ascontiguousarray(scaled.reshape(k // 512, 128, 4, n).transpose(0, 1, 3, 2))
    if fmt == "e4m3":
        words = by_word.astype(ml_dtypes.float8_e4m3fn).view(np.uint8)
    else:
        c = by_word.astype(ml_dtypes.float4_e2m1fn).view(np.uint8) & 0xF
        words = (c[..., 0::2] | (c[..., 1::2] << 4)).reshape(k // 512, 128, 2 * n)
    return np.ascontiguousarray(words), np.ascontiguousarray(byte.astype(np.uint8).reshape(k // 512, 16, n))


def unpack_weight(words, scales, fmt):
    g, _, n = scales.shape
    words = np.ascontiguousarray(words).reshape(g, 128, n, -1)
    if fmt == "e4m3":
        vals = words.view(ml_dtypes.float8_e4m3fn).astype(np.float64)
    else:
        nib = np.empty((g, 128, n, 4), np.uint8)
        nib[..., 0::2] = words & 0xF
        nib[..., 1::2] = words >> 4
        vals = E2M1[nib]
    vals = vals * np.repeat(np.exp2(scales.astype(np.float64) - 127.0), 8, axis=1)[..., None]
    return vals.transpose(0, 1, 3, 2).reshape(g * 512, n)


def d_relu(v):
    return (v > 0).astype(np.float64)


K, T, E, C, H, N = 128, 512, 8, 128, 512, 1536


def by_expert(wq, xq):
    return np.concatenate([wq[e].T @ xq[:, e * C:(e + 1) * C] for e in range(E)], axis=1)


def setup_inputs():
    n = np.random.standard_normal
    s = mx_kscale(N)[:, None]
    u = mx_kscale(H)
    first = np.random.permutation(np.repeat(np.arange(E), T // E))
    second = (first + 1 + np.random.permutation(np.repeat(np.arange(E - 1), -(-T // (E - 1)))[:T])) % E
    while np.bincount(second, minlength=E).max() != T // E:
        load = np.bincount(second, minlength=E); hi, lo = int(load.argmax()), int(load.argmin())
        t = np.flatnonzero((second == hi) & (first != lo))[0]; second[t] = lo
    slot_token = np.empty(E * C, np.int64); pos = np.empty((2, T), np.int64); fill = np.zeros(E, np.int64)
    place = np.stack([np.random.permutation(C) for _ in range(E)])
    for r, deal in enumerate((first, second)):
        for t in np.random.permutation(T):
            e = deal[t]; j = e * C + place[e, fill[e]]; fill[e] += 1; slot_token[j] = t; pos[r, t] = j
    g = np.random.uniform(0.2, 0.8, T)
    w_slot = np.empty(E * C); w_slot[pos[0]] = g; w_slot[pos[1]] = 1.0 - g
    dy = pack_weight(n((N, T)) * s, "e4m3")
    return {
        "dy_words": dy[0],
        "dy_scales": dy[1],
        "a": n((H, E * C)).astype(np.float32),
        "w2": (n((E, N, H)) / np.sqrt(N) / s[None] * u[None, None, :]).astype(np.float32),
        "w1": (n((E, H, K)) / np.sqrt(H) / u[None, :, None]).astype(np.float32),
        "gate": np.tile(w_slot, (H, 1)).astype(np.float32),
        "offs": striped(slot_token),
        "pos1": striped(pos[0]),
        "pos2": striped(pos[1]),
    }


def reference(dy_words, dy_scales, a, w2, w1, gate, offs, pos1, pos2):
    idx = unstriped(offs)
    gq = unpack_weight(dy_words, dy_scales, "e4m3")[:, idx]
    dh = f64(gate) * by_expert(mxq(f64(w2), 1, "e4m3"), gq)
    da = dh * d_relu(f64(a))
    dx = by_expert(mxq(f64(w1), 1, "e4m3"), mxq(da, 0, "e4m3"))
    return dx[:, unstriped(pos1)] + dx[:, unstriped(pos2)]

@@ -1,0 +1,256 @@
+from contextlib import ExitStack
+
+import concourse.mybir as mybir
+from concourse.masks import make_identity
+
+K, T, E, C, H, N = 128, 512, 8, 128, 512, 1536
+SLOTS = E * C
+FLOPS = 2 * SLOTS * (N * H + H * K)
+
+F32 = mybir.dt.float32
+BF16 = mybir.dt.bfloat16
+I32 = mybir.dt.int32
+U32 = mybir.dt.uint32
+U16 = mybir.dt.uint16
+U8 = mybir.dt.uint8
+FP8X4 = mybir.dt.float8_e4m3fn_x4
+ALU = mybir.AluOpType
+
+P = 128
+PACK = 4
+K_PASS = P * PACK
+PASSES = N // K_PASS
+LIST_ROWS = 16
+PAIR = 2 * C
+HALF = E // 2
+STREAM_BUFS = 14
+SCALAR_M = 96
+SCALAR_M_LAST = 40
+
+
+def tile_moe_bdx_mlp_relu_kernel(tc, dy_words, dy_scales, a, w2, w1, gate, offs, pos1, pos2, out):
+    nc = tc.nc
+    with ExitStack() as ctx:
+        keep = ctx.enter_context(tc.tile_pool(name="keep", bufs=1))
+        stream = ctx.enter_context(tc.tile_pool(name="stream", bufs=STREAM_BUFS))
+        work = ctx.enter_context(tc.tile_pool(name="work", bufs=4))
+        coded = ctx.enter_context(tc.tile_pool(name="coded", bufs=6))
+        psum = ctx.enter_context(tc.psum_pool(name="psum", bufs=3))
+
+        offs_sb = keep.tile([P, SLOTS // LIST_ROWS], U16, name="offs_sb")
+        pos1_sb = keep.tile([P, T // LIST_ROWS], U16, name="pos1_sb")
+        pos2_sb = keep.tile([P, T // LIST_ROWS], U16, name="pos2_sb")
+        dy_w = keep.tile([P, PASSES, T], I32, name="dy_w", align_bytes=64)
+        dy_s = keep.tile([P, T // 4], I32, name="dy_s", align_bytes=64)
+        g_words = keep.tile([P, PASSES, SLOTS], U32, name="g_words", align_bytes=64)
+        g_scales = keep.tile([P, SLOTS], U8, name="g_scales", align_bytes=64)
+        gate_rows = keep.tile([P, C], F32, name="gate_rows")
+        gate_cols = keep.tile([P, E], F32, name="gate_cols")
+        identity = keep.tile([P, P], F32, name="identity")
+        gate_banks = [psum.tile([P, HALF * C], F32, name="gate_bank", bufs=2) for half in range(2)]
+        gated_mask = keep.tile([P, SLOTS, PACK], F32, name="gated_mask")
+        da_codes = keep.tile([P, SLOTS], U32, name="da_codes", align_bytes=64)
+        da_scales = keep.tile([P, SLOTS], U8, name="da_scales", align_bytes=64)
+        dx = keep.tile([P, SLOTS], F32, name="dx")
+
+        def load_w2(e, o):
+            raw = stream.tile([P, PACK, H], F32, name="raw")
+            rows = w2[e, o * K_PASS:(o + 1) * K_PASS, :]
+            nc.sync.dma_start(out=raw[:], in_=rows.rearrange("(p j) i -> p j i", j=PACK))
+            return raw
+
+        def cast_w2(raw, last):
+            grouped = work.tile([P, PACK, P, PACK], BF16, name="grouped", align_bytes=64, bufs=6)
+            src = raw[:].rearrange("p j (m t) -> p m j t", t=PACK)
+            dst = grouped[:].rearrange("p t m j -> p m j t")
+            split = SCALAR_M_LAST if last else SCALAR_M
+            nc.scalar.copy(out=dst[:, :split], in_=src[:, :split])
+            nc.vector.tensor_copy(out=dst[:, split:], in_=src[:, split:])
+            return grouped
+
+        def quantize_w2(grouped, last):
+            codes = coded.tile([P, PACK, P], U32, name="codes", align_bytes=64)
+            scales = coded.tile([P, PACK, P], U8, name="scales", align_bytes=64)
+            if last:
+                for t in range(PACK):
+                    nc.vector.quantize_mx(
+                        out=codes[:, t, :].bitcast(FP8X4),
+                        scales=scales[:, t, :],
+                        in_=grouped[:, t].rearrange("p m j -> p (m j)"),
+                    )
+            else:
+                nc.vector.quantize_mx(
+                    out=codes[:].rearrange("p t m -> p (t m)").bitcast(FP8X4),
+                    scales=scales[:].rearrange("p t m -> p (t m)"),
+                    in_=grouped[:].rearrange("p t m j -> p (t m j)"),
+                )
+            return codes, scales
+
+        def gather_pair(pair):
+            cols = slice(pair * PAIR, (pair + 1) * PAIR)
+            entries = offs_sb[:, pair * PAIR // LIST_ROWS:(pair + 1) * PAIR // LIST_ROWS]
+            for o in range(PASSES):
+                nc.vector.tensor_copy(g_words[:, o, cols], dy_w[:, o, :].bitcast(U32).indirect(entries))
+            nc.vector.tensor_copy(g_scales[:, cols], dy_s[:].bitcast(U8).indirect(entries))
+
+        def spread_gate():
+            nc.sync.dma_start(out=gate_rows[:], in_=gate[0:P // E, :].rearrange("r (e s) -> (r e) s", e=E))
+            make_identity(nc, identity[:])
+            turned = psum.tile([P, P], F32, name="acc")
+            nc.tensor.transpose(turned[:], gate_rows[:], identity[:])
+            nc.scalar.copy(out=gate_cols[:], in_=turned[:, 0:E])
+            for e in range(E):
+                nc.tensor.transpose(
+                    gate_banks[e // HALF][:, (e % HALF) * C:(e % HALF + 1) * C],
+                    gate_cols[:, e:e + 1].to_broadcast([P, P]),
+                    identity[:],
+                )
+
+        def load_a(half):
+            raw = stream.tile([P, PACK, HALF * C], F32, name="raw")
+            cols = a[:, half * HALF * C:(half + 1) * HALF * C]
+            nc.sync.dma_start(out=raw[:], in_=cols.rearrange("(p t) s -> p t s", t=PACK))
+            return raw
+
+        def make_mask(raw, e):
+            cols = slice(e * C, (e + 1) * C)
+            local = slice((e % HALF) * C, (e % HALF + 1) * C)
+            nc.vector.scalar_tensor_tensor(
+                out=gated_mask[:, cols, :],
+                in0=raw[:, :, local].rearrange("p t s -> p s t"),
+                scalar=0.0,
+                in1=gate_banks[e // HALF][:, local].unsqueeze(2).to_broadcast([P, C, PACK]),
+                op0=ALU.is_gt,
+                op1=ALU.mult,
+            )
+
+        def make_dh(e, quantized):
+            cols = slice(e * C, (e + 1) * C)
+            dh = psum.tile([P, PACK, C], F32, name="dh")
+            for t in range(PACK):
+                for o in range(PASSES):
+                    codes, scales = quantized[o]
+                    nc.tensor.matmul_mx(
+                        out=dh[:, t, :],
+                        lhsT=codes[:, t, :].bitcast(FP8X4),
+                        lhsT_scale=scales[:, t, :],
+                        rhs=g_words[:, o, cols].bitcast(FP8X4),
+                        rhs_scale=g_scales[4 * o:P, cols],
+                        start=(o == 0),
+                        stop=(o == PASSES - 1),
+                    )
+            return dh
+
+        def make_da(e, dh):
+            cols = slice(e * C, (e + 1) * C)
+            da = work.tile([P, C, PACK], BF16, name="da", align_bytes=64)
+            nc.vector.tensor_tensor(
+                out=da[:], in0=dh[:].rearrange("p t s -> p s t"), in1=gated_mask[:, cols, :], op=ALU.mult
+            )
+            return da
+
+        def quantize_da(e, da):
+            cols = slice(e * C, (e + 1) * C)
+            nc.vector.quantize_mx(
+                out=da_codes[:, cols].bitcast(FP8X4),
+                scales=da_scales[:, cols],
+                in_=da[:].rearrange("p s t -> p (s t)"),
+            )
+
+        def load_w1(first, count):
+            raw = stream.tile([P, count, PACK, K], F32, name="raw")
+            rows = w1[first:first + count]
+            nc.sync.dma_start(out=raw[:], in_=rows.rearrange("e (p t) k -> p e t k", t=PACK))
+            return raw
+
+        def quantize_w1(raw, x):
+            grouped1 = work.tile([P, K, PACK], BF16, name="grouped1", align_bytes=64)
+            nc.scalar.copy(
+                out=grouped1[:].rearrange("p (c i) t -> p c t i", i=4),
+                in_=raw[:, x].rearrange("p t (c i) -> p c t i", i=4),
+            )
+            codes1 = coded.tile([P, K], U32, name="codes1", align_bytes=64)
+            scales1 = coded.tile([P, K], U8, name="scales1", align_bytes=64)
+            nc.vector.quantize_mx(
+                out=codes1[:].bitcast(FP8X4), scales=scales1[:], in_=grouped1[:].rearrange("p k t -> p (k t)")
+            )
+            return codes1, scales1
+
+        def make_dx(first, quantized):
+            count = len(quantized)
+            acc = psum.tile([P, count * C], F32, name="acc")
+            for x, (codes1, scales1) in enumerate(quantized):
+                cols = slice((first + x) * C, (first + x + 1) * C)
+                nc.tensor.matmul_mx(
+                    out=acc[:, x * C:(x + 1) * C],
+                    lhsT=codes1[:].bitcast(FP8X4),
+                    lhsT_scale=scales1[:],
+                    rhs=da_codes[:, cols].bitcast(FP8X4),
+                    rhs_scale=da_scales[:, cols],
+                    start=True,
+                    stop=True,
+                )
+            nc.scalar.copy(out=dx[:, first * C:(first + count) * C], in_=acc[:])
+
+        nc.vector.memset(dy_s[:], 0)
+        first_raw = load_w2(0, 0)
+        nc.sync.dma_start(offs_sb[:], offs)
+        nc.sync.dma_start(out=dy_w[:], in_=dy_words.rearrange("o p t d -> p o (t d)").bitcast(I32))
+        for q in range(4):
+            nc.sync.dma_start(
+                out=dy_s[32 * q:32 * q + 4 * PASSES, :], in_=dy_scales[:, 4 * q:4 * q + 4, :].bitcast(I32)
+            )
+
+        a_raw = None
+        dh = None
+        da = None
+        for e in range(E):
+            quantized = []
+            for o in range(PASSES):
+                last = (e, o) == (E - 1, PASSES - 1)
+                raw = first_raw if (e, o) == (0, 0) else load_w2(e, o)
+                if e == 0 and o == 1:
+                    spread_gate()
+                if e % HALF == 0 and o == 2:
+                    a_raw = load_a(e // HALF)
+                grouped = cast_w2(raw, last)
+                if o == 0:
+                    if e < E // 2:
+                        gather_pair(e)
+                    if e > 0:
+                        make_mask(a_raw_prev, e - 1)
+                if o == 1 and e > 0:
+                    da = make_da(e - 1, dh)
+                    if e == E - 1:
+                        make_mask(a_raw, e)
+                if o == 2 and e > 0 and not last:
+                    quantize_da(e - 1, da)
+                quantized.append(quantize_w2(grouped, last))
+                if o == 1 and e == E - 1:
+                    quantize_da(e - 1, da)
+            a_raw_prev = a_raw
+            dh = make_dh(e, quantized)
+            if e == HALF:
+                nc.sync.dma_start(pos1_sb[:], pos1)
+                nc.sync.dma_start(pos2_sb[:], pos2)
+                w1_raw = load_w1(0, HALF)
+                make_dx(0, [quantize_w1(w1_raw, x) for x in range(HALF)])
+
+        w1_raw = load_w1(4, 2)
+        early = [quantize_w1(w1_raw, x) for x in range(2)]
+        da = make_da(E - 1, dh)
+        early.append(quantize_w1(load_w1(6, 1), 0))
+        quantize_da(E - 1, da)
+        late = [quantize_w1(load_w1(7, 1), 0)]
+        make_dx(4, early)
+        make_dx(7, late)
+
+        for h in range(2):
+            entries = slice(h * T // 2 // LIST_ROWS, (h + 1) * T // 2 // LIST_ROWS)
+            first = work.tile([P, T // 2], F32, name="first")
+            second = work.tile([P, T // 2], F32, name="second")
+            nc.vector.tensor_copy(first[:], dx[:].indirect(pos1_sb[:, entries]))
+            nc.vector.tensor_copy(second[:], dx[:].indirect(pos2_sb[:, entries]))
+            total = work.tile([P, T // 2], F32, name="total")
+            nc.vector.tensor_tensor(out=total[:], in0=first[:], in1=second[:], op=ALU.add)
+            nc.sync.dma_start(out=out[:, h * T // 2:(h + 1) * T // 2], in_=total[:])

@@ -26,6 +26,7 @@ HALF = E // 2
 STREAM_BUFS = 14
 SCALAR_M = 96
 SCALAR_M_LAST = 40
+W1_ON_VECTOR = (5, 7)
 
 
 def tile_moe_bdx_mlp_relu_kernel(tc, dy_words, dy_scales, a, w2, w1, gate, offs, pos1, pos2, out):
@@ -41,6 +42,7 @@ def tile_moe_bdx_mlp_relu_kernel(tc, dy_words, dy_scales, a, w2, w1, gate, offs,
         pos1_sb = keep.tile([P, T // LIST_ROWS], U16, name="pos1_sb")
         pos2_sb = keep.tile([P, T // LIST_ROWS], U16, name="pos2_sb")
         dy_w = keep.tile([P, PASSES, T], I32, name="dy_w", align_bytes=64)
+        dy_s_rows = keep.tile([P, T // 4], I32, name="dy_s_rows")
         dy_s = keep.tile([P, T // 4], I32, name="dy_s", align_bytes=64)
         g_words = keep.tile([P, PASSES, SLOTS], U32, name="g_words", align_bytes=64)
         g_scales = keep.tile([P, SLOTS], U8, name="g_scales", align_bytes=64)
@@ -68,10 +70,10 @@ def tile_moe_bdx_mlp_relu_kernel(tc, dy_words, dy_scales, a, w2, w1, gate, offs,
             nc.vector.tensor_copy(out=dst[:, split:], in_=src[:, split:])
             return grouped
 
-        def quantize_w2(grouped, last):
+        def quantize_w2(grouped, by_tile):
             codes = coded.tile([P, PACK, P], U32, name="codes", align_bytes=64)
             scales = coded.tile([P, PACK, P], U8, name="scales", align_bytes=64)
-            if last:
+            if by_tile:
                 for t in range(PACK):
                     nc.vector.quantize_mx(
                         out=codes[:, t, :].bitcast(FP8X4),
@@ -98,7 +100,7 @@ def tile_moe_bdx_mlp_relu_kernel(tc, dy_words, dy_scales, a, w2, w1, gate, offs,
             make_identity(nc, identity[:])
             turned = psum.tile([P, P], F32, name="acc")
             nc.tensor.transpose(turned[:], gate_rows[:], identity[:])
-            nc.scalar.copy(out=gate_cols[:], in_=turned[:, 0:E])
+            nc.vector.tensor_copy(out=gate_cols[:], in_=turned[:, 0:E])
             for e in range(E):
                 nc.tensor.transpose(
                     gate_banks[e // HALF][:, (e % HALF) * C:(e % HALF + 1) * C],
@@ -112,14 +114,14 @@ def tile_moe_bdx_mlp_relu_kernel(tc, dy_words, dy_scales, a, w2, w1, gate, offs,
             nc.sync.dma_start(out=raw[:], in_=cols.rearrange("(p t) s -> p t s", t=PACK))
             return raw
 
-        def make_mask(raw, e):
-            cols = slice(e * C, (e + 1) * C)
-            local = slice((e % HALF) * C, (e % HALF + 1) * C)
+        def make_mask(raw, pair):
+            cols = slice(pair * PAIR, (pair + 1) * PAIR)
+            local = slice((pair % 2) * PAIR, (pair % 2 + 1) * PAIR)
             nc.vector.scalar_tensor_tensor(
                 out=gated_mask[:, cols, :],
                 in0=raw[:, :, local].rearrange("p t s -> p s t"),
                 scalar=0.0,
-                in1=gate_banks[e // HALF][:, local].unsqueeze(2).to_broadcast([P, C, PACK]),
+                in1=gate_banks[pair // 2][:, local].unsqueeze(2).to_broadcast([P, PAIR, PACK]),
                 op0=ALU.is_gt,
                 op1=ALU.mult,
             )
@@ -163,18 +165,24 @@ def tile_moe_bdx_mlp_relu_kernel(tc, dy_words, dy_scales, a, w2, w1, gate, offs,
             nc.sync.dma_start(out=raw[:], in_=rows.rearrange("e (p t) k -> p e t k", t=PACK))
             return raw
 
-        def quantize_w1(raw, x):
-            grouped1 = work.tile([P, K, PACK], BF16, name="grouped1", align_bytes=64)
-            nc.scalar.copy(
-                out=grouped1[:].rearrange("p (c i) t -> p c t i", i=4),
-                in_=raw[:, x].rearrange("p t (c i) -> p c t i", i=4),
-            )
-            codes1 = coded.tile([P, K], U32, name="codes1", align_bytes=64)
-            scales1 = coded.tile([P, K], U8, name="scales1", align_bytes=64)
+        def quantize_w1(first, count):
+            raw = load_w1(first, count)
+            grouped1 = work.tile([P, count, K, PACK], BF16, name="grouped1", align_bytes=64)
+            for x in range(count):
+                dst = grouped1[:, x].rearrange("p (c i) t -> p c t i", i=4)
+                src = raw[:, x].rearrange("p t (c i) -> p c t i", i=4)
+                if first + x in W1_ON_VECTOR:
+                    nc.vector.tensor_copy(out=dst, in_=src)
+                else:
+                    nc.scalar.copy(out=dst, in_=src)
+            codes1 = coded.tile([P, count, K], U32, name="codes1", align_bytes=64)
+            scales1 = coded.tile([P, count, K], U8, name="scales1", align_bytes=64)
             nc.vector.quantize_mx(
-                out=codes1[:].bitcast(FP8X4), scales=scales1[:], in_=grouped1[:].rearrange("p k t -> p (k t)")
+                out=codes1[:].rearrange("p e k -> p (e k)").bitcast(FP8X4),
+                scales=scales1[:].rearrange("p e k -> p (e k)"),
+                in_=grouped1[:].rearrange("p e k t -> p (e k t)"),
             )
-            return codes1, scales1
+            return [(codes1[:, x, :], scales1[:, x, :]) for x in range(count)]
 
         def make_dx(first, quantized):
             count = len(quantized)
@@ -183,8 +191,8 @@ def tile_moe_bdx_mlp_relu_kernel(tc, dy_words, dy_scales, a, w2, w1, gate, offs,
                 cols = slice((first + x) * C, (first + x + 1) * C)
                 nc.tensor.matmul_mx(
                     out=acc[:, x * C:(x + 1) * C],
-                    lhsT=codes1[:].bitcast(FP8X4),
-                    lhsT_scale=scales1[:],
+                    lhsT=codes1.bitcast(FP8X4),
+                    lhsT_scale=scales1,
                     rhs=da_codes[:, cols].bitcast(FP8X4),
                     rhs_scale=da_scales[:, cols],
                     start=True,
@@ -197,13 +205,12 @@ def tile_moe_bdx_mlp_relu_kernel(tc, dy_words, dy_scales, a, w2, w1, gate, offs,
         nc.sync.dma_start(offs_sb[:], offs)
         nc.sync.dma_start(out=dy_w[:], in_=dy_words.rearrange("o p t d -> p o (t d)").bitcast(I32))
         for q in range(4):
-            nc.sync.dma_start(
-                out=dy_s[32 * q:32 * q + 4 * PASSES, :], in_=dy_scales[:, 4 * q:4 * q + 4, :].bitcast(I32)
-            )
+            live = slice(32 * q, 32 * q + 4 * PASSES)
+            nc.sync.dma_start(out=dy_s_rows[live, :], in_=dy_scales[:, 4 * q:4 * q + 4, :].bitcast(I32))
+            nc.vector.tensor_copy(out=dy_s[live, :], in_=dy_s_rows[live, :])
 
         a_raw = None
         dh = None
-        da = None
         for e in range(E):
             quantized = []
             for o in range(PASSES):
@@ -211,46 +218,32 @@ def tile_moe_bdx_mlp_relu_kernel(tc, dy_words, dy_scales, a, w2, w1, gate, offs,
                 raw = first_raw if (e, o) == (0, 0) else load_w2(e, o)
                 if e == 0 and o == 1:
                     spread_gate()
-                if e % HALF == 0 and o == 2:
-                    a_raw = load_a(e // HALF)
+                if e in (0, 3) and o == 2:
+                    a_raw = load_a(e // 3)
+                    make_mask(a_raw, 2 * (e // 3))
+                    make_mask(a_raw, 2 * (e // 3) + 1)
                 grouped = cast_w2(raw, last)
-                if o == 0:
-                    if e < E // 2:
-                        gather_pair(e)
-                    if e > 0:
-                        make_mask(a_raw_prev, e - 1)
-                if o == 1 and e > 0:
-                    da = make_da(e - 1, dh)
-                    if e == E - 1:
-                        make_mask(a_raw, e)
-                if o == 2 and e > 0 and not last:
-                    quantize_da(e - 1, da)
-                quantized.append(quantize_w2(grouped, last))
-                if o == 1 and e == E - 1:
-                    quantize_da(e - 1, da)
-            a_raw_prev = a_raw
+                if o == 0 and e < E // 2:
+                    gather_pair(e)
+                if o == 0 and e > 0:
+                    quantize_da(e - 1, make_da(e - 1, dh))
+                quantized.append(quantize_w2(grouped, o == PASSES - 1))
             dh = make_dh(e, quantized)
             if e == HALF:
                 nc.sync.dma_start(pos1_sb[:], pos1)
                 nc.sync.dma_start(pos2_sb[:], pos2)
-                w1_raw = load_w1(0, HALF)
-                make_dx(0, [quantize_w1(w1_raw, x) for x in range(HALF)])
 
-        w1_raw = load_w1(4, 2)
-        early = [quantize_w1(w1_raw, x) for x in range(2)]
-        da = make_da(E - 1, dh)
-        early.append(quantize_w1(load_w1(6, 1), 0))
-        quantize_da(E - 1, da)
-        late = [quantize_w1(load_w1(7, 1), 0)]
-        make_dx(4, early)
-        make_dx(7, late)
+        quantize_da(E - 1, make_da(E - 1, dh))
+        make_dx(0, quantize_w1(0, 2) + quantize_w1(2, 2))
+        make_dx(4, quantize_w1(4, 2))
+        make_dx(6, quantize_w1(6, 1) + quantize_w1(7, 1))
 
-        for h in range(2):
-            entries = slice(h * T // 2 // LIST_ROWS, (h + 1) * T // 2 // LIST_ROWS)
-            first = work.tile([P, T // 2], F32, name="first")
-            second = work.tile([P, T // 2], F32, name="second")
+        for start, count in ((0, 384), (384, 128)):
+            entries = slice(start // LIST_ROWS, (start + count) // LIST_ROWS)
+            first = work.tile([P, count], F32, name="first", bufs=2)
+            second = work.tile([P, count], F32, name="second", bufs=2)
             nc.vector.tensor_copy(first[:], dx[:].indirect(pos1_sb[:, entries]))
             nc.vector.tensor_copy(second[:], dx[:].indirect(pos2_sb[:, entries]))
-            total = work.tile([P, T // 2], F32, name="total")
+            total = work.tile([P, count], F32, name="total", bufs=2)
             nc.vector.tensor_tensor(out=total[:], in0=first[:], in1=second[:], op=ALU.add)
-            nc.sync.dma_start(out=out[:, h * T // 2:(h + 1) * T // 2], in_=total[:])
+            nc.sync.dma_start(out=out[:, start:start + count], in_=total[:])

@@ -23,10 +23,11 @@ PASSES = N // K_PASS
 LIST_ROWS = 16
 PAIR = 2 * C
 HALF = E // 2
-STREAM_BUFS = 14
+STREAM_BUFS = 7
 SCALAR_M = 96
 SCALAR_M_LAST = 40
 W1_ON_VECTOR = (5, 7)
+DOUBLE_LOADS = range(3, 17, 2)
 
 
 def tile_moe_bdx_mlp_relu_kernel(tc, dy_words, dy_scales, a, w2, w1, gate, offs, pos1, pos2, out):
@@ -55,15 +56,16 @@ def tile_moe_bdx_mlp_relu_kernel(tc, dy_words, dy_scales, a, w2, w1, gate, offs,
         da_scales = keep.tile([P, SLOTS], U8, name="da_scales", align_bytes=64)
         dx = keep.tile([P, SLOTS], F32, name="dx")
 
-        def load_w2(e, o):
-            raw = stream.tile([P, PACK, H], F32, name="raw")
-            rows = w2[e, o * K_PASS:(o + 1) * K_PASS, :]
-            nc.sync.dma_start(out=raw[:], in_=rows.rearrange("(p j) i -> p j i", j=PACK))
-            return raw
+        w2_chunks = w2.rearrange("e (o p j) i -> p (e o) j i", p=P, j=PACK)
+
+        def load_w2(first, count):
+            raw = stream.tile([P, count, PACK, H], F32, name="raw")
+            nc.sync.dma_start(out=raw[:], in_=w2_chunks[:, first:first + count])
+            return [raw[:, x] for x in range(count)]
 
         def cast_w2(raw, last):
             grouped = work.tile([P, PACK, P, PACK], BF16, name="grouped", align_bytes=64, bufs=6)
-            src = raw[:].rearrange("p j (m t) -> p m j t", t=PACK)
+            src = raw.rearrange("p j (m t) -> p m j t", t=PACK)
             dst = grouped[:].rearrange("p t m j -> p m j t")
             split = SCALAR_M_LAST if last else SCALAR_M
             nc.scalar.copy(out=dst[:, :split], in_=src[:, :split])
@@ -108,10 +110,9 @@ def tile_moe_bdx_mlp_relu_kernel(tc, dy_words, dy_scales, a, w2, w1, gate, offs,
                     identity[:],
                 )
 
-        def load_a(half):
-            raw = stream.tile([P, PACK, HALF * C], F32, name="raw")
-            cols = a[:, half * HALF * C:(half + 1) * HALF * C]
-            nc.sync.dma_start(out=raw[:], in_=cols.rearrange("(p t) s -> p t s", t=PACK))
+        def load_a():
+            raw = stream.tile([P, PACK, SLOTS], F32, name="raw")
+            nc.sync.dma_start(out=raw[:], in_=a.rearrange("(p t) s -> p t s", t=PACK))
             return raw
 
         def make_mask(raw, pair):
@@ -119,7 +120,7 @@ def tile_moe_bdx_mlp_relu_kernel(tc, dy_words, dy_scales, a, w2, w1, gate, offs,
             local = slice((pair % 2) * PAIR, (pair % 2 + 1) * PAIR)
             nc.vector.scalar_tensor_tensor(
                 out=gated_mask[:, cols, :],
-                in0=raw[:, :, local].rearrange("p t s -> p s t"),
+                in0=raw[:, :, cols].rearrange("p t s -> p s t"),
                 scalar=0.0,
                 in1=gate_banks[pair // 2][:, local].unsqueeze(2).to_broadcast([P, PAIR, PACK]),
                 op0=ALU.is_gt,
@@ -201,28 +202,29 @@ def tile_moe_bdx_mlp_relu_kernel(tc, dy_words, dy_scales, a, w2, w1, gate, offs,
             nc.scalar.copy(out=dx[:, first * C:(first + count) * C], in_=acc[:])
 
         nc.vector.memset(dy_s[:], 0)
-        first_raw = load_w2(0, 0)
+        landed = load_w2(0, 1)
         nc.sync.dma_start(offs_sb[:], offs)
         nc.sync.dma_start(out=dy_w[:], in_=dy_words.rearrange("o p t d -> p o (t d)").bitcast(I32))
+        landed += load_w2(1, 1)
         for q in range(4):
             live = slice(32 * q, 32 * q + 4 * PASSES)
             nc.sync.dma_start(out=dy_s_rows[live, :], in_=dy_scales[:, 4 * q:4 * q + 4, :].bitcast(I32))
             nc.vector.tensor_copy(out=dy_s[live, :], in_=dy_s_rows[live, :])
 
-        a_raw = None
         dh = None
         for e in range(E):
             quantized = []
             for o in range(PASSES):
-                last = (e, o) == (E - 1, PASSES - 1)
-                raw = first_raw if (e, o) == (0, 0) else load_w2(e, o)
-                if e == 0 and o == 1:
+                chunk = e * PASSES + o
+                if chunk == len(landed):
+                    landed += load_w2(chunk, 2 if chunk in DOUBLE_LOADS else 1)
+                if chunk == 1:
                     spread_gate()
-                if e in (0, 3) and o == 2:
-                    a_raw = load_a(e // 3)
-                    make_mask(a_raw, 2 * (e // 3))
-                    make_mask(a_raw, 2 * (e // 3) + 1)
-                grouped = cast_w2(raw, last)
+                if chunk == 2:
+                    a_raw = load_a()
+                    for pair in range(E // 2):
+                        make_mask(a_raw, pair)
+                grouped = cast_w2(landed[chunk], chunk == E * PASSES - 1)
                 if o == 0 and e < E // 2:
                     gather_pair(e)
                 if o == 0 and e > 0:

@@ -23,11 +23,13 @@ PASSES = N // K_PASS
 LIST_ROWS = 16
 PAIR = 2 * C
 HALF = E // 2
-STREAM_BUFS = 7
-SCALAR_M = 96
+STREAM_BUFS = 4
+SCALAR_M_EARLY = 112
+SCALAR_M = 88
 SCALAR_M_LAST = 40
 W1_ON_VECTOR = (5, 7)
-DOUBLE_LOADS = range(3, 17, 2)
+W2_LOADS = [(3,)] * 5 + [(2, 1)] * 2 + [(1, 1, 1)]
+W1_LOADS = (2, 2, 2, 1, 1)
 
 
 def tile_moe_bdx_mlp_relu_kernel(tc, dy_words, dy_scales, a, w2, w1, gate, offs, pos1, pos2, out):
@@ -43,7 +45,6 @@ def tile_moe_bdx_mlp_relu_kernel(tc, dy_words, dy_scales, a, w2, w1, gate, offs,
         pos1_sb = keep.tile([P, T // LIST_ROWS], U16, name="pos1_sb")
         pos2_sb = keep.tile([P, T // LIST_ROWS], U16, name="pos2_sb")
         dy_w = keep.tile([P, PASSES, T], I32, name="dy_w", align_bytes=64)
-        dy_s_rows = keep.tile([P, T // 4], I32, name="dy_s_rows")
         dy_s = keep.tile([P, T // 4], I32, name="dy_s", align_bytes=64)
         g_words = keep.tile([P, PASSES, SLOTS], U32, name="g_words", align_bytes=64)
         g_scales = keep.tile([P, SLOTS], U8, name="g_scales", align_bytes=64)
@@ -58,16 +59,19 @@ def tile_moe_bdx_mlp_relu_kernel(tc, dy_words, dy_scales, a, w2, w1, gate, offs,
 
         w2_chunks = w2.rearrange("e (o p j) i -> p (e o) j i", p=P, j=PACK)
 
-        def load_w2(first, count):
-            raw = stream.tile([P, count, PACK, H], F32, name="raw")
-            nc.sync.dma_start(out=raw[:], in_=w2_chunks[:, first:first + count])
-            return [raw[:, x] for x in range(count)]
+        def load_w2(e):
+            raw = stream.tile([P, PASSES, PACK, H], F32, name="raw")
+            o = 0
+            for count in W2_LOADS[e]:
+                first = e * PASSES + o
+                nc.sync.dma_start(out=raw[:, o:o + count], in_=w2_chunks[:, first:first + count])
+                o = o + count
+            return raw
 
-        def cast_w2(raw, last):
+        def cast_w2(raw, split):
             grouped = work.tile([P, PACK, P, PACK], BF16, name="grouped", align_bytes=64, bufs=6)
             src = raw.rearrange("p j (m t) -> p m j t", t=PACK)
             dst = grouped[:].rearrange("p t m j -> p m j t")
-            split = SCALAR_M_LAST if last else SCALAR_M
             nc.scalar.copy(out=dst[:, :split], in_=src[:, :split])
             nc.vector.tensor_copy(out=dst[:, split:], in_=src[:, split:])
             return grouped
@@ -90,15 +94,17 @@ def tile_moe_bdx_mlp_relu_kernel(tc, dy_words, dy_scales, a, w2, w1, gate, offs,
                 )
             return codes, scales
 
-        def gather_pair(pair):
+        def gather_pair(pair, words):
             cols = slice(pair * PAIR, (pair + 1) * PAIR)
             entries = offs_sb[:, pair * PAIR // LIST_ROWS:(pair + 1) * PAIR // LIST_ROWS]
-            for o in range(PASSES):
-                nc.vector.tensor_copy(g_words[:, o, cols], dy_w[:, o, :].bitcast(U32).indirect(entries))
-            nc.vector.tensor_copy(g_scales[:, cols], dy_s[:].bitcast(U8).indirect(entries))
+            if words:
+                for o in range(PASSES):
+                    nc.vector.tensor_copy(g_words[:, o, cols], dy_w[:, o, :].bitcast(U32).indirect(entries))
+            else:
+                nc.vector.tensor_copy(g_scales[:, cols], dy_s[:].bitcast(U8).indirect(entries))
 
         def spread_gate():
-            nc.sync.dma_start(out=gate_rows[:], in_=gate[0:P // E, :].rearrange("r (e s) -> (r e) s", e=E))
+            nc.sync.dma_start(out=gate_rows[0:E, :], in_=gate[0:1, :].rearrange("r (e s) -> (r e) s", e=E))
             make_identity(nc, identity[:])
             turned = psum.tile([P, P], F32, name="acc")
             nc.tensor.transpose(turned[:], gate_rows[:], identity[:])
@@ -160,18 +166,20 @@ def tile_moe_bdx_mlp_relu_kernel(tc, dy_words, dy_scales, a, w2, w1, gate, offs,
                 in_=da[:].rearrange("p s t -> p (s t)"),
             )
 
-        def load_w1(first, count):
-            raw = stream.tile([P, count, PACK, K], F32, name="raw")
-            rows = w1[first:first + count]
-            nc.sync.dma_start(out=raw[:], in_=rows.rearrange("e (p t) k -> p e t k", t=PACK))
+        def load_w1():
+            raw = stream.tile([P, E, PACK, K], F32, name="raw")
+            first = 0
+            for count in W1_LOADS:
+                rows = w1[first:first + count]
+                nc.sync.dma_start(out=raw[:, first:first + count], in_=rows.rearrange("e (p t) k -> p e t k", t=PACK))
+                first = first + count
             return raw
 
-        def quantize_w1(first, count):
-            raw = load_w1(first, count)
+        def quantize_w1(raw, first, count):
             grouped1 = work.tile([P, count, K, PACK], BF16, name="grouped1", align_bytes=64)
             for x in range(count):
                 dst = grouped1[:, x].rearrange("p (c i) t -> p c t i", i=4)
-                src = raw[:, x].rearrange("p t (c i) -> p c t i", i=4)
+                src = raw[:, first + x].rearrange("p t (c i) -> p c t i", i=4)
                 if first + x in W1_ON_VECTOR:
                     nc.vector.tensor_copy(out=dst, in_=src)
                 else:
@@ -201,51 +209,54 @@ def tile_moe_bdx_mlp_relu_kernel(tc, dy_words, dy_scales, a, w2, w1, gate, offs,
                 )
             nc.scalar.copy(out=dx[:, first * C:(first + count) * C], in_=acc[:])
 
-        nc.vector.memset(dy_s[:], 0)
-        landed = load_w2(0, 1)
+        nc.gpsimd.memset(dy_s[:], 0)
+        nc.gpsimd.memset(gate_rows[:], 0.0)
         nc.sync.dma_start(offs_sb[:], offs)
         nc.sync.dma_start(out=dy_w[:], in_=dy_words.rearrange("o p t d -> p o (t d)").bitcast(I32))
-        landed += load_w2(1, 1)
+        w2_raw = load_w2(0)
         for q in range(4):
             live = slice(32 * q, 32 * q + 4 * PASSES)
-            nc.sync.dma_start(out=dy_s_rows[live, :], in_=dy_scales[:, 4 * q:4 * q + 4, :].bitcast(I32))
-            nc.vector.tensor_copy(out=dy_s[live, :], in_=dy_s_rows[live, :])
+            nc.scalar.dma_start(out=dy_s[live, :], in_=dy_scales[:, 4 * q:4 * q + 4, :].bitcast(I32))
+        for pair in range(E // 2):
+            gather_pair(pair, True)
+        for pair in range(E // 2):
+            gather_pair(pair, False)
+        spread_gate()
+        a_raw = load_a()
 
         dh = None
         for e in range(E):
+            if e > 0:
+                w2_raw = load_w2(e)
             quantized = []
             for o in range(PASSES):
-                chunk = e * PASSES + o
-                if chunk == len(landed):
-                    landed += load_w2(chunk, 2 if chunk in DOUBLE_LOADS else 1)
-                if chunk == 1:
-                    spread_gate()
-                if chunk == 2:
-                    a_raw = load_a()
-                    for pair in range(E // 2):
-                        make_mask(a_raw, pair)
-                grouped = cast_w2(landed[chunk], chunk == E * PASSES - 1)
-                if o == 0 and e < E // 2:
-                    gather_pair(e)
+                last = e == E - 1 and o == PASSES - 1
+                grouped = cast_w2(w2_raw[:, o], SCALAR_M_LAST if last else SCALAR_M_EARLY if e < 2 else SCALAR_M)
                 if o == 0 and e > 0:
                     quantize_da(e - 1, make_da(e - 1, dh))
                 quantized.append(quantize_w2(grouped, o == PASSES - 1))
             dh = make_dh(e, quantized)
+            if e == 0:
+                for pair in range(E // 2):
+                    make_mask(a_raw, pair)
             if e == HALF:
                 nc.sync.dma_start(pos1_sb[:], pos1)
                 nc.sync.dma_start(pos2_sb[:], pos2)
 
+        w1_raw = load_w1()
         quantize_da(E - 1, make_da(E - 1, dh))
-        make_dx(0, quantize_w1(0, 2) + quantize_w1(2, 2))
-        make_dx(4, quantize_w1(4, 2))
-        make_dx(6, quantize_w1(6, 1) + quantize_w1(7, 1))
+        make_dx(0, quantize_w1(w1_raw, 0, 2) + quantize_w1(w1_raw, 2, 2))
+        make_dx(4, quantize_w1(w1_raw, 4, 2))
+        make_dx(6, quantize_w1(w1_raw, 6, 1) + quantize_w1(w1_raw, 7, 1))
 
-        for start, count in ((0, 384), (384, 128)):
-            entries = slice(start // LIST_ROWS, (start + count) // LIST_ROWS)
+        pieces = ((0, 384), (384, 128))
+        firsts = []
+        for start, count in pieces:
             first = work.tile([P, count], F32, name="first", bufs=2)
-            second = work.tile([P, count], F32, name="second", bufs=2)
-            nc.vector.tensor_copy(first[:], dx[:].indirect(pos1_sb[:, entries]))
-            nc.vector.tensor_copy(second[:], dx[:].indirect(pos2_sb[:, entries]))
+            nc.vector.tensor_copy(first[:], dx[:].indirect(pos1_sb[:, start // LIST_ROWS:(start + count) // LIST_ROWS]))
+            firsts.append(first)
+        for (start, count), first in zip(pieces, firsts):
             total = work.tile([P, count], F32, name="total", bufs=2)
-            nc.vector.tensor_tensor(out=total[:], in0=first[:], in1=second[:], op=ALU.add)
+            entries = pos2_sb[:, start // LIST_ROWS:(start + count) // LIST_ROWS]
+            nc.vector.tensor_tensor(total[:], dx[:].indirect(entries), first[:], ALU.add)
             nc.sync.dma_start(out=out[:, start:start + count], in_=total[:])

@@ -26,8 +26,8 @@ HALF = E // 2
 STREAM_BUFS = 4
 SCALAR_M_EARLY = 112
 SCALAR_M = 88
-SCALAR_M_LAST = 40
-W1_ON_VECTOR = (5, 7)
+SCALAR_M_LAST = 48
+W1_ON_VECTOR = (1, 3, 6, 7)
 W2_LOADS = [(3,)] * 5 + [(2, 1)] * 2 + [(1, 1, 1)]
 W1_LOADS = (2, 2, 2, 1, 1)
 
@@ -150,11 +150,10 @@ def tile_moe_bdx_mlp_relu_kernel(tc, dy_words, dy_scales, a, w2, w1, gate, offs,
                     )
             return dh
 
-        def make_da(e, dh):
+        def make_da(e, dh, da):
             cols = slice(e * C, (e + 1) * C)
-            da = work.tile([P, C, PACK], BF16, name="da", align_bytes=64)
             nc.vector.tensor_tensor(
-                out=da[:], in0=dh[:].rearrange("p t s -> p s t"), in1=gated_mask[:, cols, :], op=ALU.mult
+                out=da, in0=dh[:].rearrange("p t s -> p s t"), in1=gated_mask[:, cols, :], op=ALU.mult
             )
             return da
 
@@ -163,7 +162,7 @@ def tile_moe_bdx_mlp_relu_kernel(tc, dy_words, dy_scales, a, w2, w1, gate, offs,
             nc.vector.quantize_mx(
                 out=da_codes[:, cols].bitcast(FP8X4),
                 scales=da_scales[:, cols],
-                in_=da[:].rearrange("p s t -> p (s t)"),
+                in_=da.rearrange("p s t -> p (s t)"),
             )
 
         def load_w1():
@@ -193,7 +192,7 @@ def tile_moe_bdx_mlp_relu_kernel(tc, dy_words, dy_scales, a, w2, w1, gate, offs,
             )
             return [(codes1[:, x, :], scales1[:, x, :]) for x in range(count)]
 
-        def make_dx(first, quantized):
+        def make_dx(first, quantized, on_vector):
             count = len(quantized)
             acc = psum.tile([P, count * C], F32, name="acc")
             for x, (codes1, scales1) in enumerate(quantized):
@@ -207,7 +206,10 @@ def tile_moe_bdx_mlp_relu_kernel(tc, dy_words, dy_scales, a, w2, w1, gate, offs,
                     start=True,
                     stop=True,
                 )
-            nc.scalar.copy(out=dx[:, first * C:(first + count) * C], in_=acc[:])
+            if on_vector:
+                nc.vector.tensor_copy(out=dx[:, first * C:(first + count) * C], in_=acc[:])
+            else:
+                nc.scalar.copy(out=dx[:, first * C:(first + count) * C], in_=acc[:])
 
         nc.gpsimd.memset(dy_s[:], 0)
         nc.gpsimd.memset(gate_rows[:], 0.0)
@@ -232,9 +234,9 @@ def tile_moe_bdx_mlp_relu_kernel(tc, dy_words, dy_scales, a, w2, w1, gate, offs,
             for o in range(PASSES):
                 last = e == E - 1 and o == PASSES - 1
                 grouped = cast_w2(w2_raw[:, o], SCALAR_M_LAST if last else SCALAR_M_EARLY if e < 2 else SCALAR_M)
+                quantized.append(quantize_w2(grouped, last))
                 if o == 0 and e > 0:
-                    quantize_da(e - 1, make_da(e - 1, dh))
-                quantized.append(quantize_w2(grouped, o == PASSES - 1))
+                    quantize_da(e - 1, make_da(e - 1, dh, grouped[:, 0]))
             dh = make_dh(e, quantized)
             if e == 0:
                 for pair in range(E // 2):
@@ -244,10 +246,14 @@ def tile_moe_bdx_mlp_relu_kernel(tc, dy_words, dy_scales, a, w2, w1, gate, offs,
                 nc.sync.dma_start(pos2_sb[:], pos2)
 
         w1_raw = load_w1()
-        quantize_da(E - 1, make_da(E - 1, dh))
-        make_dx(0, quantize_w1(w1_raw, 0, 2) + quantize_w1(w1_raw, 2, 2))
-        make_dx(4, quantize_w1(w1_raw, 4, 2))
-        make_dx(6, quantize_w1(w1_raw, 6, 1) + quantize_w1(w1_raw, 7, 1))
+        last_da = work.tile([P, C, PACK], BF16, name="last_da", align_bytes=64, bufs=1)
+        quantize_da(E - 1, make_da(E - 1, dh, last_da[:]))
+        low = quantize_w1(w1_raw, 0, 2)
+        mid = quantize_w1(w1_raw, 2, 2) + quantize_w1(w1_raw, 4, 2)
+        high = quantize_w1(w1_raw, 6, 1) + quantize_w1(w1_raw, 7, 1)
+        make_dx(0, low, False)
+        make_dx(2, mid, True)
+        make_dx(6, high, False)
 
         pieces = ((0, 384), (384, 128))
         firsts = []

@@ -24,9 +24,9 @@ LIST_ROWS = 16
 PAIR = 2 * C
 HALF = E // 2
 STREAM_BUFS = 4
-SCALAR_M_EARLY = 112
-SCALAR_M = 88
-SCALAR_M_LAST = 48
+SCALAR_M_EARLY = 104
+SCALAR_M = 76
+SCALAR_M_LAST = 44
 W1_ON_VECTOR = (1, 3, 6, 7)
 W2_LOADS = [(3,)] * 5 + [(2, 1)] * 2 + [(1, 1, 1)]
 W1_LOADS = (2, 2, 2, 1, 1)

@@ -27,9 +27,10 @@ STREAM_BUFS = 4
 SCALAR_M_EARLY = 104
 SCALAR_M = 76
 SCALAR_M_LAST = 44
-W1_ON_VECTOR = (1, 3, 6, 7)
+W1_VECTOR_K = (0, K, 0, K, 0, 64, K, 0)
+WARM_PASSES = (16, 10)
 W2_LOADS = [(3,)] * 5 + [(2, 1)] * 2 + [(1, 1, 1)]
-W1_LOADS = (2, 2, 2, 1, 1)
+W1_LOADS = ((0, 2), (2, 2), (4, 2), (6, 1), (7, 1))
 
 
 def tile_moe_bdx_mlp_relu_kernel(tc, dy_words, dy_scales, a, w2, w1, gate, offs, pos1, pos2, out):
@@ -150,6 +151,20 @@ def tile_moe_bdx_mlp_relu_kernel(tc, dy_words, dy_scales, a, w2, w1, gate, offs,
                     )
             return dh
 
+        def warm_up(e, o, count, codes, scales):
+            cols = slice(e * C, (e + 1) * C)
+            spare = psum.tile([P, PACK, C], F32, name="gate_bank", bufs=2)
+            for x in range(count):
+                nc.tensor.matmul_mx(
+                    out=spare[:, x % PACK, :],
+                    lhsT=codes[:, x % PACK, :].bitcast(FP8X4),
+                    lhsT_scale=scales[:, x % PACK, :],
+                    rhs=g_words[:, o, cols].bitcast(FP8X4),
+                    rhs_scale=g_scales[4 * o:P, cols],
+                    start=True,
+                    stop=True,
+                )
+
         def make_da(e, dh, da):
             cols = slice(e * C, (e + 1) * C)
             nc.vector.tensor_tensor(
@@ -167,22 +182,25 @@ def tile_moe_bdx_mlp_relu_kernel(tc, dy_words, dy_scales, a, w2, w1, gate, offs,
 
         def load_w1():
             raw = stream.tile([P, E, PACK, K], F32, name="raw")
-            first = 0
-            for count in W1_LOADS:
+            for first, count in W1_LOADS:
                 rows = w1[first:first + count]
                 nc.sync.dma_start(out=raw[:, first:first + count], in_=rows.rearrange("e (p t) k -> p e t k", t=PACK))
-                first = first + count
             return raw
 
-        def quantize_w1(raw, first, count):
-            grouped1 = work.tile([P, count, K, PACK], BF16, name="grouped1", align_bytes=64)
+        def cast_w1(raw, first, count):
+            grouped1 = work.tile([P, count, K, PACK], BF16, name="grouped1", align_bytes=64, bufs=5)
             for x in range(count):
                 dst = grouped1[:, x].rearrange("p (c i) t -> p c t i", i=4)
                 src = raw[:, first + x].rearrange("p t (c i) -> p c t i", i=4)
-                if first + x in W1_ON_VECTOR:
-                    nc.vector.tensor_copy(out=dst, in_=src)
-                else:
-                    nc.scalar.copy(out=dst, in_=src)
+                split = W1_VECTOR_K[first + x] // 4
+                if split > 0:
+                    nc.vector.tensor_copy(out=dst[:, :split], in_=src[:, :split])
+                if split < K // 4:
+                    nc.scalar.copy(out=dst[:, split:], in_=src[:, split:])
+            return grouped1
+
+        def quantize_w1(grouped1):
+            count = grouped1.shape[1]
             codes1 = coded.tile([P, count, K], U32, name="codes1", align_bytes=64)
             scales1 = coded.tile([P, count, K], U8, name="scales1", align_bytes=64)
             nc.vector.quantize_mx(
@@ -213,8 +231,8 @@ def tile_moe_bdx_mlp_relu_kernel(tc, dy_words, dy_scales, a, w2, w1, gate, offs,
 
         nc.gpsimd.memset(dy_s[:], 0)
         nc.gpsimd.memset(gate_rows[:], 0.0)
-        nc.sync.dma_start(offs_sb[:], offs)
         nc.sync.dma_start(out=dy_w[:], in_=dy_words.rearrange("o p t d -> p o (t d)").bitcast(I32))
+        nc.sync.dma_start(offs_sb[:], offs)
         w2_raw = load_w2(0)
         for q in range(4):
             live = slice(32 * q, 32 * q + 4 * PASSES)
@@ -235,6 +253,8 @@ def tile_moe_bdx_mlp_relu_kernel(tc, dy_words, dy_scales, a, w2, w1, gate, offs,
                 last = e == E - 1 and o == PASSES - 1
                 grouped = cast_w2(w2_raw[:, o], SCALAR_M_LAST if last else SCALAR_M_EARLY if e < 2 else SCALAR_M)
                 quantized.append(quantize_w2(grouped, last))
+                if e == E - 1 and o < PASSES - 1:
+                    warm_up(e, o, WARM_PASSES[o], *quantized[o])
                 if o == 0 and e > 0:
                     quantize_da(e - 1, make_da(e - 1, dh, grouped[:, 0]))
             dh = make_dh(e, quantized)
@@ -248,12 +268,14 @@ def tile_moe_bdx_mlp_relu_kernel(tc, dy_words, dy_scales, a, w2, w1, gate, offs,
         w1_raw = load_w1()
         last_da = work.tile([P, C, PACK], BF16, name="last_da", align_bytes=64, bufs=1)
         quantize_da(E - 1, make_da(E - 1, dh, last_da[:]))
-        low = quantize_w1(w1_raw, 0, 2)
-        mid = quantize_w1(w1_raw, 2, 2) + quantize_w1(w1_raw, 4, 2)
-        high = quantize_w1(w1_raw, 6, 1) + quantize_w1(w1_raw, 7, 1)
-        make_dx(0, low, False)
-        make_dx(2, mid, True)
-        make_dx(6, high, False)
+        rounded = [cast_w1(w1_raw, first, count) for first, count in W1_LOADS]
+        coded_w1 = {}
+        for (first, count), piece in zip(W1_LOADS, rounded):
+            for x, pair in enumerate(quantize_w1(piece)):
+                coded_w1[first + x] = pair
+        make_dx(0, [coded_w1[e] for e in (0, 1)], True)
+        make_dx(2, [coded_w1[e] for e in (2, 3, 4, 5)], False)
+        make_dx(6, [coded_w1[e] for e in (6, 7)], True)
 
         pieces = ((0, 384), (384, 128))
         firsts = []

@@ -26,8 +26,8 @@ HALF = E // 2
 STREAM_BUFS = 4
 SCALAR_M_EARLY = 104
 SCALAR_M = 76
-SCALAR_M_LAST = 44
-W1_VECTOR_K = (0, K, 0, K, 0, 64, K, 0)
+SCALAR_M_LAST = 52
+W1_VECTOR_K = (0, K, 0, 64, 0, 64, K, 0)
 WARM_PASSES = (16, 10)
 W2_LOADS = [(3,)] * 5 + [(2, 1)] * 2 + [(1, 1, 1)]
 W1_LOADS = ((0, 2), (2, 2), (4, 2), (6, 1), (7, 1))
@@ -81,11 +81,11 @@ def tile_moe_bdx_mlp_relu_kernel(tc, dy_words, dy_scales, a, w2, w1, gate, offs,
             codes = coded.tile([P, PACK, P], U32, name="codes", align_bytes=64)
             scales = coded.tile([P, PACK, P], U8, name="scales", align_bytes=64)
             if by_tile:
-                for t in range(PACK):
+                for t in range(0, PACK, 2):
                     nc.vector.quantize_mx(
-                        out=codes[:, t, :].bitcast(FP8X4),
-                        scales=scales[:, t, :],
-                        in_=grouped[:, t].rearrange("p m j -> p (m j)"),
+                        out=codes[:, t:t + 2, :].rearrange("p t m -> p (t m)").bitcast(FP8X4),
+                        scales=scales[:, t:t + 2, :].rearrange("p t m -> p (t m)"),
+                        in_=grouped[:, t:t + 2].rearrange("p t m j -> p (t m j)"),
                     )
             else:
                 nc.vector.quantize_mx(
@@ -273,7 +273,7 @@ def tile_moe_bdx_mlp_relu_kernel(tc, dy_words, dy_scales, a, w2, w1, gate, offs,
         for (first, count), piece in zip(W1_LOADS, rounded):
             for x, pair in enumerate(quantize_w1(piece)):
                 coded_w1[first + x] = pair
-        make_dx(0, [coded_w1[e] for e in (0, 1)], True)
+        make_dx(0, [coded_w1[e] for e in (0, 1)], False)
         make_dx(2, [coded_w1[e] for e in (2, 3, 4, 5)], False)
         make_dx(6, [coded_w1[e] for e in (6, 7)], True)
 

@@ -26,10 +26,10 @@ HALF = E // 2
 STREAM_BUFS = 4
 SCALAR_M_EARLY = 104
 SCALAR_M = 76
-SCALAR_M_LAST = 52
+SCALAR_M_LAST = 104
 W1_VECTOR_K = (0, K, 0, 64, 0, 64, K, 0)
-WARM_PASSES = (16, 10)
-W2_LOADS = [(3,)] * 5 + [(2, 1)] * 2 + [(1, 1, 1)]
+WARM_PASSES = (4, 2)
+W2_LOADS = [(3,)] * 5 + [(2, 1)] + [(1, 1, 1)] * 2
 W1_LOADS = ((0, 2), (2, 2), (4, 2), (6, 1), (7, 1))
 
 
@@ -69,12 +69,17 @@ def tile_moe_bdx_mlp_relu_kernel(tc, dy_words, dy_scales, a, w2, w1, gate, offs,
                 o = o + count
             return raw
 
-        def cast_w2(raw, split):
+        def cast_w2(raw, split, by_tile):
             grouped = work.tile([P, PACK, P, PACK], BF16, name="grouped", align_bytes=64, bufs=6)
             src = raw.rearrange("p j (m t) -> p m j t", t=PACK)
             dst = grouped[:].rearrange("p t m j -> p m j t")
-            nc.scalar.copy(out=dst[:, :split], in_=src[:, :split])
-            nc.vector.tensor_copy(out=dst[:, split:], in_=src[:, split:])
+            if by_tile:
+                nc.scalar.copy(out=dst[:, :split, :, 2:], in_=src[:, :split, :, 2:])
+                nc.vector.tensor_copy(out=dst[:, :, :, :2], in_=src[:, :, :, :2])
+                nc.vector.tensor_copy(out=dst[:, split:, :, 2:], in_=src[:, split:, :, 2:])
+            else:
+                nc.scalar.copy(out=dst[:, :split], in_=src[:, :split])
+                nc.vector.tensor_copy(out=dst[:, split:], in_=src[:, split:])
             return grouped
 
         def quantize_w2(grouped, by_tile):
@@ -152,11 +157,11 @@ def tile_moe_bdx_mlp_relu_kernel(tc, dy_words, dy_scales, a, w2, w1, gate, offs,
             return dh
 
         def warm_up(e, o, count, codes, scales):
-            cols = slice(e * C, (e + 1) * C)
-            spare = psum.tile([P, PACK, C], F32, name="gate_bank", bufs=2)
+            cols = slice(0, HALF * C)
+            spare = psum.tile([P, HALF * C], F32, name="gate_bank", bufs=2)
             for x in range(count):
                 nc.tensor.matmul_mx(
-                    out=spare[:, x % PACK, :],
+                    out=spare[:],
                     lhsT=codes[:, x % PACK, :].bitcast(FP8X4),
                     lhsT_scale=scales[:, x % PACK, :],
                     rhs=g_words[:, o, cols].bitcast(FP8X4),
@@ -251,7 +256,7 @@ def tile_moe_bdx_mlp_relu_kernel(tc, dy_words, dy_scales, a, w2, w1, gate, offs,
             quantized = []
             for o in range(PASSES):
                 last = e == E - 1 and o == PASSES - 1
-                grouped = cast_w2(w2_raw[:, o], SCALAR_M_LAST if last else SCALAR_M_EARLY if e < 2 else SCALAR_M)
+                grouped = cast_w2(w2_raw[:, o], SCALAR_M_LAST if last else SCALAR_M_EARLY if e < 2 else SCALAR_M, last)
                 quantized.append(quantize_w2(grouped, last))
                 if e == E - 1 and o < PASSES - 1:
                     warm_up(e, o, WARM_PASSES[o], *quantized[o])

@@ -266,11 +266,10 @@ def tile_moe_bdx_mlp_relu_kernel(tc, dy_words, dy_scales, a, w2, w1, gate, offs,
             if e == 0:
                 for pair in range(E // 2):
                     make_mask(a_raw, pair)
-            if e == HALF:
-                nc.sync.dma_start(pos1_sb[:], pos1)
-                nc.sync.dma_start(pos2_sb[:], pos2)
 
         w1_raw = load_w1()
+        nc.sync.dma_start(pos1_sb[:], pos1)
+        nc.sync.dma_start(pos2_sb[:], pos2)
         last_da = work.tile([P, C, PACK], BF16, name="last_da", align_bytes=64, bufs=1)
         quantize_da(E - 1, make_da(E - 1, dh, last_da[:]))
         rounded = [cast_w1(w1_raw, first, count) for first, count in W1_LOADS]

@@ -27,7 +27,7 @@ STREAM_BUFS = 4
 SCALAR_M_EARLY = 104
 SCALAR_M = 76
 SCALAR_M_LAST = 104
-W1_VECTOR_K = (0, K, 0, 64, 0, 64, K, 0)
+W1_VECTOR_K = (0, K, 0, 0, 0, K, K, 80)
 WARM_PASSES = (4, 2)
 W2_LOADS = [(3,)] * 5 + [(2, 1)] + [(1, 1, 1)] * 2
 W1_LOADS = ((0, 2), (2, 2), (4, 2), (6, 1), (7, 1))
@@ -208,11 +208,12 @@ def tile_moe_bdx_mlp_relu_kernel(tc, dy_words, dy_scales, a, w2, w1, gate, offs,
             count = grouped1.shape[1]
             codes1 = coded.tile([P, count, K], U32, name="codes1", align_bytes=64)
             scales1 = coded.tile([P, count, K], U8, name="scales1", align_bytes=64)
-            nc.vector.quantize_mx(
-                out=codes1[:].rearrange("p e k -> p (e k)").bitcast(FP8X4),
-                scales=scales1[:].rearrange("p e k -> p (e k)"),
-                in_=grouped1[:].rearrange("p e k t -> p (e k t)"),
-            )
+            for x in range(count):
+                nc.vector.quantize_mx(
+                    out=codes1[:, x, :].bitcast(FP8X4),
+                    scales=scales1[:, x, :],
+                    in_=grouped1[:, x].rearrange("p k t -> p (k t)"),
+                )
             return [(codes1[:, x, :], scales1[:, x, :]) for x in range(count)]
 
         def make_dx(first, quantized, on_vector):
@@ -277,9 +278,8 @@ def tile_moe_bdx_mlp_relu_kernel(tc, dy_words, dy_scales, a, w2, w1, gate, offs,
         for (first, count), piece in zip(W1_LOADS, rounded):
             for x, pair in enumerate(quantize_w1(piece)):
                 coded_w1[first + x] = pair
-        make_dx(0, [coded_w1[e] for e in (0, 1)], False)
-        make_dx(2, [coded_w1[e] for e in (2, 3, 4, 5)], False)
-        make_dx(6, [coded_w1[e] for e in (6, 7)], True)
+        for group in ((0, 1), (2, 3), (4, 5, 6), (7,)):
+            make_dx(group[0], [coded_w1[e] for e in group], False)
 
         pieces = ((0, 384), (384, 128))
         firsts = []

@@ -27,7 +27,7 @@ STREAM_BUFS = 4
 SCALAR_M_EARLY = 104
 SCALAR_M = 76
 SCALAR_M_LAST = 104
-W1_VECTOR_K = (0, K, 0, 0, 0, K, K, 80)
+W1_VECTOR_K = (0, K, 0, 0, K, K, 0, 64)
 WARM_PASSES = (4, 2)
 W2_LOADS = [(3,)] * 5 + [(2, 1)] + [(1, 1, 1)] * 2
 W1_LOADS = ((0, 2), (2, 2), (4, 2), (6, 1), (7, 1))
@@ -56,7 +56,6 @@ def tile_moe_bdx_mlp_relu_kernel(tc, dy_words, dy_scales, a, w2, w1, gate, offs,
         gated_mask = keep.tile([P, SLOTS, PACK], F32, name="gated_mask")
         da_codes = keep.tile([P, SLOTS], U32, name="da_codes", align_bytes=64)
         da_scales = keep.tile([P, SLOTS], U8, name="da_scales", align_bytes=64)
-        dx = keep.tile([P, SLOTS], F32, name="dx")
 
         w2_chunks = w2.rearrange("e (o p j) i -> p (e o) j i", p=P, j=PACK)
 
@@ -86,11 +85,11 @@ def tile_moe_bdx_mlp_relu_kernel(tc, dy_words, dy_scales, a, w2, w1, gate, offs,
             codes = coded.tile([P, PACK, P], U32, name="codes", align_bytes=64)
             scales = coded.tile([P, PACK, P], U8, name="scales", align_bytes=64)
             if by_tile:
-                for t in range(0, PACK, 2):
+                for tiles in (slice(0, 2), slice(2, 3), slice(3, 4)):
                     nc.vector.quantize_mx(
-                        out=codes[:, t:t + 2, :].rearrange("p t m -> p (t m)").bitcast(FP8X4),
-                        scales=scales[:, t:t + 2, :].rearrange("p t m -> p (t m)"),
-                        in_=grouped[:, t:t + 2].rearrange("p t m j -> p (t m j)"),
+                        out=codes[:, tiles, :].rearrange("p t m -> p (t m)").bitcast(FP8X4),
+                        scales=scales[:, tiles, :].rearrange("p t m -> p (t m)"),
+                        in_=grouped[:, tiles].rearrange("p t m j -> p (t m j)"),
                     )
             else:
                 nc.vector.quantize_mx(
@@ -193,7 +192,10 @@ def tile_moe_bdx_mlp_relu_kernel(tc, dy_words, dy_scales, a, w2, w1, gate, offs,
             return raw
 
         def cast_w1(raw, first, count):
-            grouped1 = work.tile([P, count, K, PACK], BF16, name="grouped1", align_bytes=64, bufs=5)
+            if first == E - 1:
+                grouped1 = keep.tile([P, count, K, PACK], BF16, name="dx", align_bytes=64)
+            else:
+                grouped1 = work.tile([P, count, K, PACK], BF16, name="grouped1", align_bytes=64, bufs=4)
             for x in range(count):
                 dst = grouped1[:, x].rearrange("p (c i) t -> p c t i", i=4)
                 src = raw[:, first + x].rearrange("p t (c i) -> p c t i", i=4)
@@ -218,7 +220,7 @@ def tile_moe_bdx_mlp_relu_kernel(tc, dy_words, dy_scales, a, w2, w1, gate, offs,
 
         def make_dx(first, quantized, on_vector):
             count = len(quantized)
-            acc = psum.tile([P, count * C], F32, name="acc")
+            acc = psum.tile([P, count * C], F32, name="dh" if on_vector else "acc")
             for x, (codes1, scales1) in enumerate(quantized):
                 cols = slice((first + x) * C, (first + x + 1) * C)
                 nc.tensor.matmul_mx(
@@ -278,8 +280,9 @@ def tile_moe_bdx_mlp_relu_kernel(tc, dy_words, dy_scales, a, w2, w1, gate, offs,
         for (first, count), piece in zip(W1_LOADS, rounded):
             for x, pair in enumerate(quantize_w1(piece)):
                 coded_w1[first + x] = pair
-        for group in ((0, 1), (2, 3), (4, 5, 6), (7,)):
-            make_dx(group[0], [coded_w1[e] for e in group], False)
+        dx = keep.tile([P, SLOTS], F32, name="dx", align_bytes=64)
+        for group in ((0, 1, 2, 3), (4, 5), (6,), (7,)):
+            make_dx(group[0], [coded_w1[e] for e in group], group[0] == 0)
 
         pieces = ((0, 384), (384, 128))
         firsts = []

@@ -27,7 +27,7 @@ STREAM_BUFS = 4
 SCALAR_M_EARLY = 104
 SCALAR_M = 76
 SCALAR_M_LAST = 104
-W1_VECTOR_K = (0, K, 0, 0, K, K, 0, 64)
+W1_VECTOR_K = (0, K, 0, 0, 64, K, 0, 64)
 WARM_PASSES = (4, 2)
 W2_LOADS = [(3,)] * 5 + [(2, 1)] + [(1, 1, 1)] * 2
 W1_LOADS = ((0, 2), (2, 2), (4, 2), (6, 1), (7, 1))
@@ -184,21 +184,19 @@ def tile_moe_bdx_mlp_relu_kernel(tc, dy_words, dy_scales, a, w2, w1, gate, offs,
                 in_=da.rearrange("p s t -> p (s t)"),
             )
 
-        def load_w1():
-            raw = stream.tile([P, E, PACK, K], F32, name="raw")
-            for first, count in W1_LOADS:
-                rows = w1[first:first + count]
-                nc.sync.dma_start(out=raw[:, first:first + count], in_=rows.rearrange("e (p t) k -> p e t k", t=PACK))
-            return raw
+        def load_w1(first, count):
+            if first == E - 1:
+                raw1 = keep.tile([P, count, PACK, K], F32, name="dx")
+            else:
+                raw1 = work.tile([P, count, PACK, K], F32, name="raw1", bufs=len(W1_LOADS) - 1)
+            nc.sync.dma_start(out=raw1[:], in_=w1[first:first + count].rearrange("e (p t) k -> p e t k", t=PACK))
+            return raw1
 
         def cast_w1(raw, first, count):
-            if first == E - 1:
-                grouped1 = keep.tile([P, count, K, PACK], BF16, name="dx", align_bytes=64)
-            else:
-                grouped1 = work.tile([P, count, K, PACK], BF16, name="grouped1", align_bytes=64, bufs=4)
+            grouped1 = work.tile([P, count, K, PACK], BF16, name="grouped1", align_bytes=64, bufs=5)
             for x in range(count):
                 dst = grouped1[:, x].rearrange("p (c i) t -> p c t i", i=4)
-                src = raw[:, first + x].rearrange("p t (c i) -> p c t i", i=4)
+                src = raw[:, x].rearrange("p t (c i) -> p c t i", i=4)
                 split = W1_VECTOR_K[first + x] // 4
                 if split > 0:
                     nc.vector.tensor_copy(out=dst[:, :split], in_=src[:, :split])
@@ -270,19 +268,19 @@ def tile_moe_bdx_mlp_relu_kernel(tc, dy_words, dy_scales, a, w2, w1, gate, offs,
                 for pair in range(E // 2):
                     make_mask(a_raw, pair)
 
-        w1_raw = load_w1()
+        w1_raw = [load_w1(first, count) for first, count in W1_LOADS]
         nc.sync.dma_start(pos1_sb[:], pos1)
         nc.sync.dma_start(pos2_sb[:], pos2)
         last_da = work.tile([P, C, PACK], BF16, name="last_da", align_bytes=64, bufs=1)
         quantize_da(E - 1, make_da(E - 1, dh, last_da[:]))
-        rounded = [cast_w1(w1_raw, first, count) for first, count in W1_LOADS]
+        rounded = [cast_w1(raw1, first, count) for (first, count), raw1 in zip(W1_LOADS, w1_raw)]
         coded_w1 = {}
         for (first, count), piece in zip(W1_LOADS, rounded):
             for x, pair in enumerate(quantize_w1(piece)):
                 coded_w1[first + x] = pair
-        dx = keep.tile([P, SLOTS], F32, name="dx", align_bytes=64)
-        for group in ((0, 1, 2, 3), (4, 5), (6,), (7,)):
-            make_dx(group[0], [coded_w1[e] for e in group], group[0] == 0)
+        dx = keep.tile([P, SLOTS], F32, name="dx")
+        for group in ((0, 1, 2, 3), (4,), (5, 6), (7,)):
+            make_dx(group[0], [coded_w1[e] for e in group], group[0] == 5)
 
         pieces = ((0, 384), (384, 128))
         firsts = []

@@ -29,7 +29,7 @@ SCALAR_M = 76
 SCALAR_M_LAST = 104
 W1_VECTOR_K = (0, K, 0, 0, 64, K, 0, 64)
 WARM_PASSES = (4, 2)
-W2_LOADS = [(3,)] * 5 + [(2, 1)] + [(1, 1, 1)] * 2
+W2_LOADS = [(3,)] * 4 + [(2, 1)] + [(1, 1, 1)] * 3
 W1_LOADS = ((0, 2), (2, 2), (4, 2), (6, 1), (7, 1))
 
 

@@ -20,16 +20,15 @@ P = 128
 PACK = 4
 K_PASS = P * PACK
 PASSES = N // K_PASS
+CHUNKS = E * PASSES
 LIST_ROWS = 16
 PAIR = 2 * C
 HALF = E // 2
-STREAM_BUFS = 4
+RING = 8
 SCALAR_M_EARLY = 104
 SCALAR_M = 76
 SCALAR_M_LAST = 104
 W1_VECTOR_K = (0, K, 0, 0, 64, K, 0, 64)
-WARM_PASSES = (4, 2)
-W2_LOADS = [(3,)] * 4 + [(2, 1)] + [(1, 1, 1)] * 3
 W1_LOADS = ((0, 2), (2, 2), (4, 2), (6, 1), (7, 1))
 
 
@@ -37,9 +36,8 @@ def tile_moe_bdx_mlp_relu_kernel(tc, dy_words, dy_scales, a, w2, w1, gate, offs,
     nc = tc.nc
     with ExitStack() as ctx:
         keep = ctx.enter_context(tc.tile_pool(name="keep", bufs=1))
-        stream = ctx.enter_context(tc.tile_pool(name="stream", bufs=STREAM_BUFS))
+        ring = ctx.enter_context(tc.tile_pool(name="ring", bufs=RING))
         work = ctx.enter_context(tc.tile_pool(name="work", bufs=4))
-        coded = ctx.enter_context(tc.tile_pool(name="coded", bufs=6))
         psum = ctx.enter_context(tc.psum_pool(name="psum", bufs=3))
 
         offs_sb = keep.tile([P, SLOTS // LIST_ROWS], U16, name="offs_sb")
@@ -53,24 +51,21 @@ def tile_moe_bdx_mlp_relu_kernel(tc, dy_words, dy_scales, a, w2, w1, gate, offs,
         gate_cols = keep.tile([P, E], F32, name="gate_cols")
         identity = keep.tile([P, P], F32, name="identity")
         gate_banks = [psum.tile([P, HALF * C], F32, name="gate_bank", bufs=2) for half in range(2)]
+        a_raw = keep.tile([P, PACK, SLOTS], F32, name="a_raw")
         gated_mask = keep.tile([P, SLOTS, PACK], F32, name="gated_mask")
         da_codes = keep.tile([P, SLOTS], U32, name="da_codes", align_bytes=64)
         da_scales = keep.tile([P, SLOTS], U8, name="da_scales", align_bytes=64)
 
         w2_chunks = w2.rearrange("e (o p j) i -> p (e o) j i", p=P, j=PACK)
 
-        def load_w2(e):
-            raw = stream.tile([P, PASSES, PACK, H], F32, name="raw")
-            o = 0
-            for count in W2_LOADS[e]:
-                first = e * PASSES + o
-                nc.sync.dma_start(out=raw[:, o:o + count], in_=w2_chunks[:, first:first + count])
-                o = o + count
+        def load_chunk(c):
+            raw = ring.tile([P, PACK, H], F32, name="raw")
+            nc.sync.dma_start(out=raw[:], in_=w2_chunks[:, c])
             return raw
 
-        def cast_w2(raw, split, by_tile):
-            grouped = work.tile([P, PACK, P, PACK], BF16, name="grouped", align_bytes=64, bufs=6)
-            src = raw.rearrange("p j (m t) -> p m j t", t=PACK)
+        def round_chunk(raw, split, by_tile):
+            grouped = work.tile([P, PACK, P, PACK], BF16, name="grouped", align_bytes=64)
+            src = raw[:].rearrange("p j (m t) -> p m j t", t=PACK)
             dst = grouped[:].rearrange("p t m j -> p m j t")
             if by_tile:
                 nc.scalar.copy(out=dst[:, :split, :, 2:], in_=src[:, :split, :, 2:])
@@ -81,23 +76,29 @@ def tile_moe_bdx_mlp_relu_kernel(tc, dy_words, dy_scales, a, w2, w1, gate, offs,
                 nc.vector.tensor_copy(out=dst[:, split:], in_=src[:, split:])
             return grouped
 
-        def quantize_w2(grouped, by_tile):
-            codes = coded.tile([P, PACK, P], U32, name="codes", align_bytes=64)
-            scales = coded.tile([P, PACK, P], U8, name="scales", align_bytes=64)
-            if by_tile:
-                for tiles in (slice(0, 2), slice(2, 3), slice(3, 4)):
-                    nc.vector.quantize_mx(
-                        out=codes[:, tiles, :].rearrange("p t m -> p (t m)").bitcast(FP8X4),
-                        scales=scales[:, tiles, :].rearrange("p t m -> p (t m)"),
-                        in_=grouped[:, tiles].rearrange("p t m j -> p (t m j)"),
-                    )
-            else:
+        def quantize_chunk(grouped, by_tile):
+            codes = work.tile([P, PACK, P], U32, name="codes", align_bytes=64)
+            scales = work.tile([P, PACK, P], U8, name="scales", align_bytes=64)
+            for tiles in (slice(0, 2), slice(2, 4)) if by_tile else (slice(0, PACK),):
                 nc.vector.quantize_mx(
-                    out=codes[:].rearrange("p t m -> p (t m)").bitcast(FP8X4),
-                    scales=scales[:].rearrange("p t m -> p (t m)"),
-                    in_=grouped[:].rearrange("p t m j -> p (t m j)"),
+                    out=codes[:, tiles, :].rearrange("p t m -> p (t m)").bitcast(FP8X4),
+                    scales=scales[:, tiles, :].rearrange("p t m -> p (t m)"),
+                    in_=grouped[:, tiles].rearrange("p t m j -> p (t m j)"),
                 )
             return codes, scales
+
+        def add_chunk(dh, e, o, codes, scales):
+            cols = slice(e * C, (e + 1) * C)
+            for t in range(PACK):
+                nc.tensor.matmul_mx(
+                    out=dh[:, t, :],
+                    lhsT=codes[:, t, :].bitcast(FP8X4),
+                    lhsT_scale=scales[:, t, :],
+                    rhs=g_words[:, o, cols].bitcast(FP8X4),
+                    rhs_scale=g_scales[4 * o:P, cols],
+                    start=(o == 0 and t == 0),
+                    stop=(o == PASSES - 1 and t == PACK - 1),
+                )
 
         def gather_pair(pair, words):
             cols = slice(pair * PAIR, (pair + 1) * PAIR)
@@ -121,67 +122,28 @@ def tile_moe_bdx_mlp_relu_kernel(tc, dy_words, dy_scales, a, w2, w1, gate, offs,
                     identity[:],
                 )
 
-        def load_a():
-            raw = stream.tile([P, PACK, SLOTS], F32, name="raw")
-            nc.sync.dma_start(out=raw[:], in_=a.rearrange("(p t) s -> p t s", t=PACK))
-            return raw
-
-        def make_mask(raw, pair):
+        def make_mask(pair):
             cols = slice(pair * PAIR, (pair + 1) * PAIR)
             local = slice((pair % 2) * PAIR, (pair % 2 + 1) * PAIR)
             nc.vector.scalar_tensor_tensor(
                 out=gated_mask[:, cols, :],
-                in0=raw[:, :, cols].rearrange("p t s -> p s t"),
+                in0=a_raw[:, :, cols].rearrange("p t s -> p s t"),
                 scalar=0.0,
                 in1=gate_banks[pair // 2][:, local].unsqueeze(2).to_broadcast([P, PAIR, PACK]),
                 op0=ALU.is_gt,
                 op1=ALU.mult,
             )
 
-        def make_dh(e, quantized):
+        def make_da(e, dh):
             cols = slice(e * C, (e + 1) * C)
-            dh = psum.tile([P, PACK, C], F32, name="dh")
-            for t in range(PACK):
-                for o in range(PASSES):
-                    codes, scales = quantized[o]
-                    nc.tensor.matmul_mx(
-                        out=dh[:, t, :],
-                        lhsT=codes[:, t, :].bitcast(FP8X4),
-                        lhsT_scale=scales[:, t, :],
-                        rhs=g_words[:, o, cols].bitcast(FP8X4),
-                        rhs_scale=g_scales[4 * o:P, cols],
-                        start=(o == 0),
-                        stop=(o == PASSES - 1),
-                    )
-            return dh
-
-        def warm_up(e, o, count, codes, scales):
-            cols = slice(0, HALF * C)
-            spare = psum.tile([P, HALF * C], F32, name="gate_bank", bufs=2)
-            for x in range(count):
-                nc.tensor.matmul_mx(
-                    out=spare[:],
-                    lhsT=codes[:, x % PACK, :].bitcast(FP8X4),
-                    lhsT_scale=scales[:, x % PACK, :],
-                    rhs=g_words[:, o, cols].bitcast(FP8X4),
-                    rhs_scale=g_scales[4 * o:P, cols],
-                    start=True,
-                    stop=True,
-                )
-
-        def make_da(e, dh, da):
-            cols = slice(e * C, (e + 1) * C)
+            da = work.tile([P, C, PACK], BF16, name="da", align_bytes=64, bufs=2)
             nc.vector.tensor_tensor(
-                out=da, in0=dh[:].rearrange("p t s -> p s t"), in1=gated_mask[:, cols, :], op=ALU.mult
+                out=da[:], in0=dh[:].rearrange("p t s -> p s t"), in1=gated_mask[:, cols, :], op=ALU.mult
             )
-            return da
-
-        def quantize_da(e, da):
-            cols = slice(e * C, (e + 1) * C)
             nc.vector.quantize_mx(
                 out=da_codes[:, cols].bitcast(FP8X4),
                 scales=da_scales[:, cols],
-                in_=da.rearrange("p s t -> p (s t)"),
+                in_=da[:].rearrange("p s t -> p (s t)"),
             )
 
         def load_w1(first, count):
@@ -192,7 +154,7 @@ def tile_moe_bdx_mlp_relu_kernel(tc, dy_words, dy_scales, a, w2, w1, gate, offs,
             nc.sync.dma_start(out=raw1[:], in_=w1[first:first + count].rearrange("e (p t) k -> p e t k", t=PACK))
             return raw1
 
-        def cast_w1(raw, first, count):
+        def round_w1(raw, first, count):
             grouped1 = work.tile([P, count, K, PACK], BF16, name="grouped1", align_bytes=64, bufs=5)
             for x in range(count):
                 dst = grouped1[:, x].rearrange("p (c i) t -> p c t i", i=4)
@@ -206,8 +168,8 @@ def tile_moe_bdx_mlp_relu_kernel(tc, dy_words, dy_scales, a, w2, w1, gate, offs,
 
         def quantize_w1(grouped1):
             count = grouped1.shape[1]
-            codes1 = coded.tile([P, count, K], U32, name="codes1", align_bytes=64)
-            scales1 = coded.tile([P, count, K], U8, name="scales1", align_bytes=64)
+            codes1 = work.tile([P, count, K], U32, name="codes1", align_bytes=64, bufs=5)
+            scales1 = work.tile([P, count, K], U8, name="scales1", align_bytes=64, bufs=5)
             for x in range(count):
                 nc.vector.quantize_mx(
                     out=codes1[:, x, :].bitcast(FP8X4),
@@ -239,41 +201,35 @@ def tile_moe_bdx_mlp_relu_kernel(tc, dy_words, dy_scales, a, w2, w1, gate, offs,
         nc.gpsimd.memset(gate_rows[:], 0.0)
         nc.sync.dma_start(out=dy_w[:], in_=dy_words.rearrange("o p t d -> p o (t d)").bitcast(I32))
         nc.sync.dma_start(offs_sb[:], offs)
-        w2_raw = load_w2(0)
+        raws = [load_chunk(0)]
         for q in range(4):
             live = slice(32 * q, 32 * q + 4 * PASSES)
             nc.scalar.dma_start(out=dy_s[live, :], in_=dy_scales[:, 4 * q:4 * q + 4, :].bitcast(I32))
+        raws.extend(load_chunk(c) for c in range(1, PASSES))
         for pair in range(E // 2):
             gather_pair(pair, True)
         for pair in range(E // 2):
             gather_pair(pair, False)
         spread_gate()
-        a_raw = load_a()
+        nc.sync.dma_start(out=a_raw[:], in_=a.rearrange("(p t) s -> p t s", t=PACK))
 
-        dh = None
         for e in range(E):
-            if e > 0:
-                w2_raw = load_w2(e)
-            quantized = []
+            dh = psum.tile([P, PACK, C], F32, name="dh")
             for o in range(PASSES):
-                last = e == E - 1 and o == PASSES - 1
-                grouped = cast_w2(w2_raw[:, o], SCALAR_M_LAST if last else SCALAR_M_EARLY if e < 2 else SCALAR_M, last)
-                quantized.append(quantize_w2(grouped, last))
-                if e == E - 1 and o < PASSES - 1:
-                    warm_up(e, o, WARM_PASSES[o], *quantized[o])
-                if o == 0 and e > 0:
-                    quantize_da(e - 1, make_da(e - 1, dh, grouped[:, 0]))
-            dh = make_dh(e, quantized)
+                c = e * PASSES + o
+                raw = raws[c] if c < len(raws) else load_chunk(c)
+                last = c == CHUNKS - 1
+                grouped = round_chunk(raw, SCALAR_M_LAST if last else SCALAR_M_EARLY if e < 2 else SCALAR_M, last)
+                add_chunk(dh, e, o, *quantize_chunk(grouped, last))
             if e == 0:
                 for pair in range(E // 2):
-                    make_mask(a_raw, pair)
+                    make_mask(pair)
+            make_da(e, dh)
 
         w1_raw = [load_w1(first, count) for first, count in W1_LOADS]
         nc.sync.dma_start(pos1_sb[:], pos1)
         nc.sync.dma_start(pos2_sb[:], pos2)
-        last_da = work.tile([P, C, PACK], BF16, name="last_da", align_bytes=64, bufs=1)
-        quantize_da(E - 1, make_da(E - 1, dh, last_da[:]))
-        rounded = [cast_w1(raw1, first, count) for (first, count), raw1 in zip(W1_LOADS, w1_raw)]
+        rounded = [round_w1(raw1, first, count) for (first, count), raw1 in zip(W1_LOADS, w1_raw)]
         coded_w1 = {}
         for (first, count), piece in zip(W1_LOADS, rounded):
             for x, pair in enumerate(quantize_w1(piece)):

@@ -26,6 +26,7 @@ PAIR = 2 * C
 HALF = E // 2
 RING = 8
 SCALAR_M_EARLY = 104
+SCALAR_M_FIRST = 64
 SCALAR_M = 76
 SCALAR_M_LAST = 104
 W1_VECTOR_K = (0, K, 0, 0, 64, K, 0, 64)
@@ -59,7 +60,7 @@ def tile_moe_bdx_mlp_relu_kernel(tc, dy_words, dy_scales, a, w2, w1, gate, offs,
         w2_chunks = w2.rearrange("e (o p j) i -> p (e o) j i", p=P, j=PACK)
 
         def load_chunk(c):
-            raw = ring.tile([P, PACK, H], F32, name="raw")
+            raw = ring.tile([P, PACK, H], F32, name="raw", align_bytes=64)
             nc.sync.dma_start(out=raw[:], in_=w2_chunks[:, c])
             return raw
 
@@ -73,7 +74,8 @@ def tile_moe_bdx_mlp_relu_kernel(tc, dy_words, dy_scales, a, w2, w1, gate, offs,
                 nc.vector.tensor_copy(out=dst[:, split:, :, 2:], in_=src[:, split:, :, 2:])
             else:
                 nc.scalar.copy(out=dst[:, :split], in_=src[:, :split])
-                nc.vector.tensor_copy(out=dst[:, split:], in_=src[:, split:])
+                if split < P:
+                    nc.vector.tensor_copy(out=dst[:, split:], in_=src[:, split:])
             return grouped
 
         def quantize_chunk(grouped, by_tile):
@@ -134,17 +136,17 @@ def tile_moe_bdx_mlp_relu_kernel(tc, dy_words, dy_scales, a, w2, w1, gate, offs,
                 op1=ALU.mult,
             )
 
-        def make_da(e, dh):
-            cols = slice(e * C, (e + 1) * C)
-            da = work.tile([P, C, PACK], BF16, name="da", align_bytes=64, bufs=2)
+        def make_da(e, dh, da):
             nc.vector.tensor_tensor(
-                out=da[:], in0=dh[:].rearrange("p t s -> p s t"), in1=gated_mask[:, cols, :], op=ALU.mult
+                out=da.rearrange("p (s t) -> p s t", t=PACK),
+                in0=dh[:].rearrange("p t s -> p s t"),
+                in1=gated_mask[:, e * C:(e + 1) * C, :],
+                op=ALU.mult,
             )
-            nc.vector.quantize_mx(
-                out=da_codes[:, cols].bitcast(FP8X4),
-                scales=da_scales[:, cols],
-                in_=da[:].rearrange("p s t -> p (s t)"),
-            )
+
+        def quantize_da(e, da):
+            cols = slice(e * C, (e + 1) * C)
+            nc.vector.quantize_mx(out=da_codes[:, cols].bitcast(FP8X4), scales=da_scales[:, cols], in_=da)
 
         def load_w1(first, count):
             if first == E - 1:
@@ -213,18 +215,33 @@ def tile_moe_bdx_mlp_relu_kernel(tc, dy_words, dy_scales, a, w2, w1, gate, offs,
         spread_gate()
         nc.sync.dma_start(out=a_raw[:], in_=a.rearrange("(p t) s -> p t s", t=PACK))
 
+        dh = None
         for e in range(E):
+            dh_before = dh
             dh = psum.tile([P, PACK, C], F32, name="dh")
             for o in range(PASSES):
                 c = e * PASSES + o
                 raw = raws[c] if c < len(raws) else load_chunk(c)
                 last = c == CHUNKS - 1
-                grouped = round_chunk(raw, SCALAR_M_LAST if last else SCALAR_M_EARLY if e < 2 else SCALAR_M, last)
+                if e == 0:
+                    split = P
+                elif o == 0:
+                    split = SCALAR_M_FIRST
+                else:
+                    split = SCALAR_M_LAST if last else SCALAR_M_EARLY if e == 1 else SCALAR_M
+                grouped = round_chunk(raw, split, last)
+                if e > 0 and o == 0:
+                    da = raw[:, PACK - 1, SCALAR_M_FIRST * PACK:].bitcast(BF16)
+                    make_da(e - 1, dh_before, da)
                 add_chunk(dh, e, o, *quantize_chunk(grouped, last))
+                if e > 0 and o == 0:
+                    quantize_da(e - 1, da)
             if e == 0:
                 for pair in range(E // 2):
                     make_mask(pair)
-            make_da(e, dh)
+        last_da = work.tile([P, C * PACK], BF16, name="last_da", align_bytes=64, bufs=1)
+        make_da(E - 1, dh, last_da[:])
+        quantize_da(E - 1, last_da[:])
 
         w1_raw = [load_w1(first, count) for first, count in W1_LOADS]
         nc.sync.dma_start(pos1_sb[:], pos1)

@@ -255,7 +255,7 @@ def tile_moe_bdx_mlp_relu_kernel(tc, dy_words, dy_scales, a, w2, w1, gate, offs,
         for group in ((0, 1, 2, 3), (4,), (5, 6), (7,)):
             make_dx(group[0], [coded_w1[e] for e in group], group[0] == 5)
 
-        pieces = ((0, 384), (384, 128))
+        pieces = ((0, 320), (320, 192))
         firsts = []
         for start, count in pieces:
             first = work.tile([P, count], F32, name="first", bufs=2)

@@ -168,16 +168,18 @@ def tile_moe_bdx_mlp_relu_kernel(tc, dy_words, dy_scales, a, w2, w1, gate, offs,
                     nc.scalar.copy(out=dst[:, split:], in_=src[:, split:])
             return grouped1
 
-        def quantize_w1(grouped1):
+        def quantize_w1(grouped1, parts):
             count = grouped1.shape[1]
             codes1 = work.tile([P, count, K], U32, name="codes1", align_bytes=64, bufs=5)
             scales1 = work.tile([P, count, K], U8, name="scales1", align_bytes=64, bufs=5)
             for x in range(count):
-                nc.vector.quantize_mx(
-                    out=codes1[:, x, :].bitcast(FP8X4),
-                    scales=scales1[:, x, :],
-                    in_=grouped1[:, x].rearrange("p k t -> p (k t)"),
-                )
+                for part in range(parts):
+                    ks = slice(part * K // parts, (part + 1) * K // parts)
+                    nc.vector.quantize_mx(
+                        out=codes1[:, x, ks].bitcast(FP8X4),
+                        scales=scales1[:, x, ks],
+                        in_=grouped1[:, x, ks].rearrange("p k t -> p (k t)"),
+                    )
             return [(codes1[:, x, :], scales1[:, x, :]) for x in range(count)]
 
         def make_dx(first, quantized, on_vector):
@@ -249,7 +251,7 @@ def tile_moe_bdx_mlp_relu_kernel(tc, dy_words, dy_scales, a, w2, w1, gate, offs,
         rounded = [round_w1(raw1, first, count) for (first, count), raw1 in zip(W1_LOADS, w1_raw)]
         coded_w1 = {}
         for (first, count), piece in zip(W1_LOADS, rounded):
-            for x, pair in enumerate(quantize_w1(piece)):
+            for x, pair in enumerate(quantize_w1(piece, 2 if first == E - 1 else 1)):
                 coded_w1[first + x] = pair
         dx = keep.tile([P, SLOTS], F32, name="dx")
         for group in ((0, 1, 2, 3), (4,), (5, 6), (7,)):

@@ -15,6 +15,7 @@ U16 = mybir.dt.uint16
 U8 = mybir.dt.uint8
 FP8X4 = mybir.dt.float8_e4m3fn_x4
 ALU = mybir.AluOpType
+COPY = mybir.ActivationFunctionType.Copy
 
 P = 128
 PACK = 4
@@ -24,20 +25,24 @@ CHUNKS = E * PASSES
 LIST_ROWS = 16
 PAIR = 2 * C
 HALF = E // 2
-RING = 8
+CHUNK_BYTES = PACK * H * 4
+W1_BYTES = PACK * K * 4
+PLACES = 8
+W2_LOADS = (1,) * CHUNKS
 SCALAR_M_EARLY = 104
 SCALAR_M_FIRST = 64
 SCALAR_M = 76
 SCALAR_M_LAST = 104
 W1_VECTOR_K = (0, K, 0, 0, 64, K, 0, 64)
 W1_LOADS = ((0, 2), (2, 2), (4, 2), (6, 1), (7, 1))
+PIECE = 160
 
 
 def tile_moe_bdx_mlp_relu_kernel(tc, dy_words, dy_scales, a, w2, w1, gate, offs, pos1, pos2, out):
     nc = tc.nc
     with ExitStack() as ctx:
         keep = ctx.enter_context(tc.tile_pool(name="keep", bufs=1))
-        ring = ctx.enter_context(tc.tile_pool(name="ring", bufs=RING))
+        ring = ctx.enter_context(tc.tile_pool(name="ring", bufs=1))
         work = ctx.enter_context(tc.tile_pool(name="work", bufs=4))
         psum = ctx.enter_context(tc.psum_pool(name="psum", bufs=3))
 
@@ -58,20 +63,26 @@ def tile_moe_bdx_mlp_relu_kernel(tc, dy_words, dy_scales, a, w2, w1, gate, offs,
         da_scales = keep.tile([P, SLOTS], U8, name="da_scales", align_bytes=64)
 
         w2_chunks = w2.rearrange("e (o p j) i -> p (e o) j i", p=P, j=PACK)
+        raws = []
 
-        def load_chunk(c):
-            raw = ring.tile([P, PACK, H], F32, name="raw", align_bytes=64)
-            nc.sync.dma_start(out=raw[:], in_=w2_chunks[:, c])
-            return raw
+        def load_chunks(count):
+            first = len(raws)
+            raw = ring.tile(
+                [P, count, PACK, H], F32, name="raw%d" % first, align_bytes=64, offset=(first % PLACES) * CHUNK_BYTES
+            )
+            nc.sync.dma_start(out=raw[:], in_=w2_chunks[:, first:first + count])
+            raws.extend(raw[:, x] for x in range(count))
 
-        def round_chunk(raw, split, by_tile):
+        def round_chunk(raw, split, by_tile, first):
             grouped = work.tile([P, PACK, P, PACK], BF16, name="grouped", align_bytes=64)
-            src = raw[:].rearrange("p j (m t) -> p m j t", t=PACK)
+            src = raw.rearrange("p j (m t) -> p m j t", t=PACK)
             dst = grouped[:].rearrange("p t m j -> p m j t")
             if by_tile:
                 nc.scalar.copy(out=dst[:, :split, :, 2:], in_=src[:, :split, :, 2:])
                 nc.vector.tensor_copy(out=dst[:, :, :, :2], in_=src[:, :, :, :2])
                 nc.vector.tensor_copy(out=dst[:, split:, :, 2:], in_=src[:, split:, :, 2:])
+            elif first:
+                nc.scalar.activation(out=dst, in_=src, func=COPY)
             else:
                 nc.scalar.copy(out=dst[:, :split], in_=src[:, :split])
                 if split < P:
@@ -152,7 +163,7 @@ def tile_moe_bdx_mlp_relu_kernel(tc, dy_words, dy_scales, a, w2, w1, gate, offs,
             if first == E - 1:
                 raw1 = keep.tile([P, count, PACK, K], F32, name="dx")
             else:
-                raw1 = work.tile([P, count, PACK, K], F32, name="raw1", bufs=len(W1_LOADS) - 1)
+                raw1 = ring.tile([P, count, PACK, K], F32, name="raw1_%d" % first, align_bytes=64, offset=first * W1_BYTES)
             nc.sync.dma_start(out=raw1[:], in_=w1[first:first + count].rearrange("e (p t) k -> p e t k", t=PACK))
             return raw1
 
@@ -205,11 +216,12 @@ def tile_moe_bdx_mlp_relu_kernel(tc, dy_words, dy_scales, a, w2, w1, gate, offs,
         nc.gpsimd.memset(gate_rows[:], 0.0)
         nc.sync.dma_start(out=dy_w[:], in_=dy_words.rearrange("o p t d -> p o (t d)").bitcast(I32))
         nc.sync.dma_start(offs_sb[:], offs)
-        raws = [load_chunk(0)]
+        load_chunks(W2_LOADS[0])
         for q in range(4):
             live = slice(32 * q, 32 * q + 4 * PASSES)
             nc.scalar.dma_start(out=dy_s[live, :], in_=dy_scales[:, 4 * q:4 * q + 4, :].bitcast(I32))
-        raws.extend(load_chunk(c) for c in range(1, PASSES))
+        load_chunks(W2_LOADS[1])
+        load_chunks(W2_LOADS[2])
         for pair in range(E // 2):
             gather_pair(pair, True)
         for pair in range(E // 2):
@@ -217,13 +229,16 @@ def tile_moe_bdx_mlp_relu_kernel(tc, dy_words, dy_scales, a, w2, w1, gate, offs,
         spread_gate()
         nc.sync.dma_start(out=a_raw[:], in_=a.rearrange("(p t) s -> p t s", t=PACK))
 
+        later_loads = list(W2_LOADS[3:])
         dh = None
         for e in range(E):
             dh_before = dh
             dh = psum.tile([P, PACK, C], F32, name="dh")
             for o in range(PASSES):
                 c = e * PASSES + o
-                raw = raws[c] if c < len(raws) else load_chunk(c)
+                if c == len(raws):
+                    load_chunks(later_loads.pop(0))
+                raw = raws[c]
                 last = c == CHUNKS - 1
                 if e == 0:
                     split = P
@@ -231,7 +246,7 @@ def tile_moe_bdx_mlp_relu_kernel(tc, dy_words, dy_scales, a, w2, w1, gate, offs,
                     split = SCALAR_M_FIRST
                 else:
                     split = SCALAR_M_LAST if last else SCALAR_M_EARLY if e == 1 else SCALAR_M
-                grouped = round_chunk(raw, split, last)
+                grouped = round_chunk(raw, split, last, c == 0)
                 if e > 0 and o == 0:
                     da = raw[:, PACK - 1, SCALAR_M_FIRST * PACK:].bitcast(BF16)
                     make_da(e - 1, dh_before, da)
@@ -257,14 +272,21 @@ def tile_moe_bdx_mlp_relu_kernel(tc, dy_words, dy_scales, a, w2, w1, gate, offs,
         for group in ((0, 1, 2, 3), (4,), (5, 6), (7,)):
             make_dx(group[0], [coded_w1[e] for e in group], group[0] == 5)
 
-        pieces = ((0, 320), (320, 192))
+        def fetched(pos_sb, tokens):
+            return dx[:].indirect(pos_sb[:, tokens.start // LIST_ROWS:tokens.stop // LIST_ROWS])
+
+        pieces = (slice(0, PIECE), slice(PIECE, 2 * PIECE), slice(2 * PIECE, T))
         firsts = []
-        for start, count in pieces:
-            first = work.tile([P, count], F32, name="first", bufs=2)
-            nc.vector.tensor_copy(first[:], dx[:].indirect(pos1_sb[:, start // LIST_ROWS:(start + count) // LIST_ROWS]))
+        for tokens in pieces:
+            first = keep.tile([P, tokens.stop - tokens.start], F32, name="first%d" % tokens.start)
+            nc.scalar.activation(out=first[:], in_=fetched(pos1_sb, tokens), func=COPY)
             firsts.append(first)
-        for (start, count), first in zip(pieces, firsts):
-            total = work.tile([P, count], F32, name="total", bufs=2)
-            entries = pos2_sb[:, start // LIST_ROWS:(start + count) // LIST_ROWS]
-            nc.vector.tensor_tensor(total[:], dx[:].indirect(entries), first[:], ALU.add)
-            nc.sync.dma_start(out=out[:, start:start + count], in_=total[:])
+        second = keep.tile([P, T - 2 * PIECE], F32, name="second")
+        early = keep.tile([P, 2 * PIECE], F32, name="early")
+        late = keep.tile([P, T - 2 * PIECE], F32, name="late")
+        nc.vector.tensor_copy(second[:], fetched(pos2_sb, pieces[2]))
+        for tokens, first in zip(pieces[:2], firsts):
+            nc.vector.tensor_tensor(early[:, tokens], fetched(pos2_sb, tokens), first[:], ALU.add)
+        nc.sync.dma_start(out=out[:, :2 * PIECE], in_=early[:])
+        nc.vector.tensor_tensor(late[:], second[:], firsts[2][:], ALU.add)
+        nc.sync.dma_start(out=out[:, pieces[2]], in_=late[:])

@@ -27,9 +27,8 @@ PAIR = 2 * C
 HALF = E // 2
 CHUNK_BYTES = PACK * H * 4
 W1_BYTES = PACK * K * 4
-PLACES = 8
-W2_LOADS = (1,) * CHUNKS
-SCALAR_M_EARLY = 104
+PLACES = 12
+W2_LOADS = (1, 1, 1, 3, 3, 3, 2, 2, 2, 1, 1, 1, 1, 1, 1)
 SCALAR_M_FIRST = 64
 SCALAR_M = 76
 SCALAR_M_LAST = 104
@@ -245,7 +244,7 @@ def tile_moe_bdx_mlp_relu_kernel(tc, dy_words, dy_scales, a, w2, w1, gate, offs,
                 elif o == 0:
                     split = SCALAR_M_FIRST
                 else:
-                    split = SCALAR_M_LAST if last else SCALAR_M_EARLY if e == 1 else SCALAR_M
+                    split = SCALAR_M_LAST if last else SCALAR_M
                 grouped = round_chunk(raw, split, last, c == 0)
                 if e > 0 and o == 0:
                     da = raw[:, PACK - 1, SCALAR_M_FIRST * PACK:].bitcast(BF16)

@@ -34,7 +34,8 @@ SCALAR_M = 76
 SCALAR_M_LAST = 104
 W1_VECTOR_K = (0, K, 0, 0, 64, K, 0, 64)
 W1_LOADS = ((0, 2), (2, 2), (4, 2), (6, 1), (7, 1))
-PIECE = 160
+PLAIN_END = 160
+OWN_END = 320
 
 
 def tile_moe_bdx_mlp_relu_kernel(tc, dy_words, dy_scales, a, w2, w1, gate, offs, pos1, pos2, out):
@@ -274,18 +275,19 @@ def tile_moe_bdx_mlp_relu_kernel(tc, dy_words, dy_scales, a, w2, w1, gate, offs,
         def fetched(pos_sb, tokens):
             return dx[:].indirect(pos_sb[:, tokens.start // LIST_ROWS:tokens.stop // LIST_ROWS])
 
-        pieces = (slice(0, PIECE), slice(PIECE, 2 * PIECE), slice(2 * PIECE, T))
-        firsts = []
-        for tokens in pieces:
-            first = keep.tile([P, tokens.stop - tokens.start], F32, name="first%d" % tokens.start)
-            nc.scalar.activation(out=first[:], in_=fetched(pos1_sb, tokens), func=COPY)
-            firsts.append(first)
-        second = keep.tile([P, T - 2 * PIECE], F32, name="second")
-        early = keep.tile([P, 2 * PIECE], F32, name="early")
-        late = keep.tile([P, T - 2 * PIECE], F32, name="late")
-        nc.vector.tensor_copy(second[:], fetched(pos2_sb, pieces[2]))
-        for tokens, first in zip(pieces[:2], firsts):
-            nc.vector.tensor_tensor(early[:, tokens], fetched(pos2_sb, tokens), first[:], ALU.add)
-        nc.sync.dma_start(out=out[:, :2 * PIECE], in_=early[:])
-        nc.vector.tensor_tensor(late[:], second[:], firsts[2][:], ALU.add)
-        nc.sync.dma_start(out=out[:, pieces[2]], in_=late[:])
+        plain, own, closing = slice(0, PLAIN_END), slice(PLAIN_END, OWN_END), slice(OWN_END, T)
+        first_plain = keep.tile([P, PLAIN_END], F32, name="first_plain")
+        first_own = keep.tile([P, OWN_END - PLAIN_END], F32, name="first_own")
+        first_closing = keep.tile([P, T - OWN_END], F32, name="first_closing")
+        second_plain = keep.tile([P, PLAIN_END], F32, name="second_plain")
+        early = keep.tile([P, OWN_END], F32, name="early")
+        late = keep.tile([P, T - OWN_END], F32, name="late")
+        nc.scalar.activation(out=first_plain[:], in_=fetched(pos1_sb, plain), func=COPY)
+        nc.scalar.activation(out=first_closing[:], in_=fetched(pos1_sb, closing), func=COPY)
+        nc.vector.tensor_copy(first_own[:], fetched(pos1_sb, own))
+        nc.vector.tensor_copy(second_plain[:], fetched(pos2_sb, plain))
+        nc.vector.tensor_tensor(early[:, own], fetched(pos2_sb, own), first_own[:], ALU.add)
+        nc.vector.tensor_tensor(early[:, plain], second_plain[:], first_plain[:], ALU.add)
+        nc.sync.dma_start(out=out[:, :OWN_END], in_=early[:])
+        nc.vector.tensor_tensor(late[:], fetched(pos2_sb, closing), first_closing[:], ALU.add)
+        nc.sync.dma_start(out=out[:, closing], in_=late[:])

@@ -28,6 +28,7 @@ HALF = E // 2
 CHUNK_BYTES = PACK * H * 4
 W1_BYTES = PACK * K * 4
 PLACES = 12
+DMA_ALIGN = 256
 W2_LOADS = (1, 1, 1, 3, 3, 3, 2, 2, 2, 1, 1, 1, 1, 1, 1)
 SCALAR_M_FIRST = 64
 SCALAR_M = 76
@@ -49,15 +50,15 @@ def tile_moe_bdx_mlp_relu_kernel(tc, dy_words, dy_scales, a, w2, w1, gate, offs,
         offs_sb = keep.tile([P, SLOTS // LIST_ROWS], U16, name="offs_sb")
         pos1_sb = keep.tile([P, T // LIST_ROWS], U16, name="pos1_sb")
         pos2_sb = keep.tile([P, T // LIST_ROWS], U16, name="pos2_sb")
-        dy_w = keep.tile([P, PASSES, T], I32, name="dy_w", align_bytes=64)
-        dy_s = keep.tile([P, T // 4], I32, name="dy_s", align_bytes=64)
+        dy_w = keep.tile([P, PASSES, T], I32, name="dy_w", align_bytes=DMA_ALIGN)
+        dy_s = keep.tile([P, T // 4], I32, name="dy_s", align_bytes=DMA_ALIGN)
         g_words = keep.tile([P, PASSES, SLOTS], U32, name="g_words", align_bytes=64)
         g_scales = keep.tile([P, SLOTS], U8, name="g_scales", align_bytes=64)
-        gate_rows = keep.tile([P, C], F32, name="gate_rows")
+        gate_rows = keep.tile([P, C], F32, name="gate_rows", align_bytes=DMA_ALIGN)
         gate_cols = keep.tile([P, E], F32, name="gate_cols")
         identity = keep.tile([P, P], F32, name="identity")
         gate_banks = [psum.tile([P, HALF * C], F32, name="gate_bank", bufs=2) for half in range(2)]
-        a_raw = keep.tile([P, PACK, SLOTS], F32, name="a_raw")
+        a_raw = keep.tile([P, PACK, SLOTS], F32, name="a_raw", align_bytes=DMA_ALIGN)
         gated_mask = keep.tile([P, SLOTS, PACK], F32, name="gated_mask")
         da_codes = keep.tile([P, SLOTS], U32, name="da_codes", align_bytes=64)
         da_scales = keep.tile([P, SLOTS], U8, name="da_scales", align_bytes=64)
@@ -68,7 +69,7 @@ def tile_moe_bdx_mlp_relu_kernel(tc, dy_words, dy_scales, a, w2, w1, gate, offs,
         def load_chunks(count):
             first = len(raws)
             raw = ring.tile(
-                [P, count, PACK, H], F32, name="raw%d" % first, align_bytes=64, offset=(first % PLACES) * CHUNK_BYTES
+                [P, count, PACK, H], F32, name="raw%d" % first, align_bytes=DMA_ALIGN, offset=(first % PLACES) * CHUNK_BYTES
             )
             nc.sync.dma_start(out=raw[:], in_=w2_chunks[:, first:first + count])
             raws.extend(raw[:, x] for x in range(count))
@@ -161,9 +162,9 @@ def tile_moe_bdx_mlp_relu_kernel(tc, dy_words, dy_scales, a, w2, w1, gate, offs,
 
         def load_w1(first, count):
             if first == E - 1:
-                raw1 = keep.tile([P, count, PACK, K], F32, name="dx")
+                raw1 = keep.tile([P, count, PACK, K], F32, name="dx", align_bytes=DMA_ALIGN)
             else:
-                raw1 = ring.tile([P, count, PACK, K], F32, name="raw1_%d" % first, align_bytes=64, offset=first * W1_BYTES)
+                raw1 = ring.tile([P, count, PACK, K], F32, name="raw1_%d" % first, align_bytes=DMA_ALIGN, offset=first * W1_BYTES)
             nc.sync.dma_start(out=raw1[:], in_=w1[first:first + count].rearrange("e (p t) k -> p e t k", t=PACK))
             return raw1
 
@@ -268,7 +269,7 @@ def tile_moe_bdx_mlp_relu_kernel(tc, dy_words, dy_scales, a, w2, w1, gate, offs,
         for (first, count), piece in zip(W1_LOADS, rounded):
             for x, pair in enumerate(quantize_w1(piece, 2 if first == E - 1 else 1)):
                 coded_w1[first + x] = pair
-        dx = keep.tile([P, SLOTS], F32, name="dx")
+        dx = keep.tile([P, SLOTS], F32, name="dx", align_bytes=DMA_ALIGN)
         for group in ((0, 1, 2, 3), (4,), (5, 6), (7,)):
             make_dx(group[0], [coded_w1[e] for e in group], group[0] == 5)
 
@@ -280,8 +281,8 @@ def tile_moe_bdx_mlp_relu_kernel(tc, dy_words, dy_scales, a, w2, w1, gate, offs,
         first_own = keep.tile([P, OWN_END - PLAIN_END], F32, name="first_own")
         first_closing = keep.tile([P, T - OWN_END], F32, name="first_closing")
         second_plain = keep.tile([P, PLAIN_END], F32, name="second_plain")
-        early = keep.tile([P, OWN_END], F32, name="early")
-        late = keep.tile([P, T - OWN_END], F32, name="late")
+        early = keep.tile([P, OWN_END], F32, name="early", align_bytes=DMA_ALIGN)
+        late = keep.tile([P, T - OWN_END], F32, name="late", align_bytes=DMA_ALIGN)
         nc.scalar.activation(out=first_plain[:], in_=fetched(pos1_sb, plain), func=COPY)
         nc.scalar.activation(out=first_closing[:], in_=fetched(pos1_sb, closing), func=COPY)
         nc.vector.tensor_copy(first_own[:], fetched(pos1_sb, own))

@@ -28,7 +28,8 @@ HALF = E // 2
 CHUNK_BYTES = PACK * H * 4
 W1_BYTES = PACK * K * 4
 PLACES = 12
-DMA_ALIGN = 256
+DMA_ALIGN = 4096
+SMALL_ALIGN = 256
 W2_LOADS = (1, 1, 1, 3, 3, 3, 2, 2, 2, 1, 1, 1, 1, 1, 1)
 SCALAR_M_FIRST = 64
 SCALAR_M = 76
@@ -47,14 +48,14 @@ def tile_moe_bdx_mlp_relu_kernel(tc, dy_words, dy_scales, a, w2, w1, gate, offs,
         work = ctx.enter_context(tc.tile_pool(name="work", bufs=4))
         psum = ctx.enter_context(tc.psum_pool(name="psum", bufs=3))
 
-        offs_sb = keep.tile([P, SLOTS // LIST_ROWS], U16, name="offs_sb")
-        pos1_sb = keep.tile([P, T // LIST_ROWS], U16, name="pos1_sb")
-        pos2_sb = keep.tile([P, T // LIST_ROWS], U16, name="pos2_sb")
+        offs_sb = keep.tile([P, SLOTS // LIST_ROWS], U16, name="offs_sb", align_bytes=SMALL_ALIGN)
+        pos1_sb = keep.tile([P, T // LIST_ROWS], U16, name="pos1_sb", align_bytes=SMALL_ALIGN)
+        pos2_sb = keep.tile([P, T // LIST_ROWS], U16, name="pos2_sb", align_bytes=SMALL_ALIGN)
         dy_w = keep.tile([P, PASSES, T], I32, name="dy_w", align_bytes=DMA_ALIGN)
-        dy_s = keep.tile([P, T // 4], I32, name="dy_s", align_bytes=DMA_ALIGN)
+        dy_s = keep.tile([P, T // 4], I32, name="dy_s", align_bytes=SMALL_ALIGN)
         g_words = keep.tile([P, PASSES, SLOTS], U32, name="g_words", align_bytes=64)
         g_scales = keep.tile([P, SLOTS], U8, name="g_scales", align_bytes=64)
-        gate_rows = keep.tile([P, C], F32, name="gate_rows", align_bytes=DMA_ALIGN)
+        gate_rows = keep.tile([P, C], F32, name="gate_rows", align_bytes=SMALL_ALIGN)
         gate_cols = keep.tile([P, E], F32, name="gate_cols")
         identity = keep.tile([P, P], F32, name="identity")
         gate_banks = [psum.tile([P, HALF * C], F32, name="gate_bank", bufs=2) for half in range(2)]
@@ -281,8 +282,8 @@ def tile_moe_bdx_mlp_relu_kernel(tc, dy_words, dy_scales, a, w2, w1, gate, offs,
         first_own = keep.tile([P, OWN_END - PLAIN_END], F32, name="first_own")
         first_closing = keep.tile([P, T - OWN_END], F32, name="first_closing")
         second_plain = keep.tile([P, PLAIN_END], F32, name="second_plain")
-        early = keep.tile([P, OWN_END], F32, name="early", align_bytes=DMA_ALIGN)
-        late = keep.tile([P, T - OWN_END], F32, name="late", align_bytes=DMA_ALIGN)
+        early = keep.tile([P, OWN_END], F32, name="early", align_bytes=SMALL_ALIGN)
+        late = keep.tile([P, T - OWN_END], F32, name="late", align_bytes=SMALL_ALIGN)
         nc.scalar.activation(out=first_plain[:], in_=fetched(pos1_sb, plain), func=COPY)
         nc.scalar.activation(out=first_closing[:], in_=fetched(pos1_sb, closing), func=COPY)
         nc.vector.tensor_copy(first_own[:], fetched(pos1_sb, own))

@@ -28,14 +28,13 @@ HALF = E // 2
 CHUNK_BYTES = PACK * H * 4
 W1_BYTES = PACK * K * 4
 PLACES = 12
-DMA_ALIGN = 4096
-SMALL_ALIGN = 256
-W2_LOADS = (1, 1, 1, 3, 3, 3, 2, 2, 2, 1, 1, 1, 1, 1, 1)
+DMA_ALIGN = 256
+W2_LOADS = (1, 1, 1, 3, 3, 3, 3, 2, 2, 1, 1, 1, 1, 1)
 SCALAR_M_FIRST = 64
 SCALAR_M = 76
 SCALAR_M_LAST = 104
 W1_VECTOR_K = (0, K, 0, 0, 64, K, 0, 64)
-W1_LOADS = ((0, 2), (2, 2), (4, 2), (6, 1), (7, 1))
+W1_LOADS = ((0, 2), (2, 2), (4, 1), (5, 1), (6, 1), (7, 1))
 PLAIN_END = 160
 OWN_END = 320
 
@@ -48,14 +47,14 @@ def tile_moe_bdx_mlp_relu_kernel(tc, dy_words, dy_scales, a, w2, w1, gate, offs,
         work = ctx.enter_context(tc.tile_pool(name="work", bufs=4))
         psum = ctx.enter_context(tc.psum_pool(name="psum", bufs=3))
 
-        offs_sb = keep.tile([P, SLOTS // LIST_ROWS], U16, name="offs_sb", align_bytes=SMALL_ALIGN)
-        pos1_sb = keep.tile([P, T // LIST_ROWS], U16, name="pos1_sb", align_bytes=SMALL_ALIGN)
-        pos2_sb = keep.tile([P, T // LIST_ROWS], U16, name="pos2_sb", align_bytes=SMALL_ALIGN)
+        offs_sb = keep.tile([P, SLOTS // LIST_ROWS], U16, name="offs_sb", align_bytes=DMA_ALIGN)
+        pos1_sb = keep.tile([P, T // LIST_ROWS], U16, name="pos1_sb", align_bytes=DMA_ALIGN)
+        pos2_sb = keep.tile([P, T // LIST_ROWS], U16, name="pos2_sb", align_bytes=DMA_ALIGN)
         dy_w = keep.tile([P, PASSES, T], I32, name="dy_w", align_bytes=DMA_ALIGN)
-        dy_s = keep.tile([P, T // 4], I32, name="dy_s", align_bytes=SMALL_ALIGN)
+        dy_s = keep.tile([P, T // 4], I32, name="dy_s", align_bytes=DMA_ALIGN)
         g_words = keep.tile([P, PASSES, SLOTS], U32, name="g_words", align_bytes=64)
         g_scales = keep.tile([P, SLOTS], U8, name="g_scales", align_bytes=64)
-        gate_rows = keep.tile([P, C], F32, name="gate_rows", align_bytes=SMALL_ALIGN)
+        gate_rows = keep.tile([P, C], F32, name="gate_rows", align_bytes=DMA_ALIGN)
         gate_cols = keep.tile([P, E], F32, name="gate_cols")
         identity = keep.tile([P, P], F32, name="identity")
         gate_banks = [psum.tile([P, HALF * C], F32, name="gate_bank", bufs=2) for half in range(2)]
@@ -170,7 +169,7 @@ def tile_moe_bdx_mlp_relu_kernel(tc, dy_words, dy_scales, a, w2, w1, gate, offs,
             return raw1
 
         def round_w1(raw, first, count):
-            grouped1 = work.tile([P, count, K, PACK], BF16, name="grouped1", align_bytes=64, bufs=5)
+            grouped1 = work.tile([P, count, K, PACK], BF16, name="grouped1", align_bytes=64, bufs=len(W1_LOADS))
             for x in range(count):
                 dst = grouped1[:, x].rearrange("p (c i) t -> p c t i", i=4)
                 src = raw[:, x].rearrange("p t (c i) -> p c t i", i=4)
@@ -183,8 +182,8 @@ def tile_moe_bdx_mlp_relu_kernel(tc, dy_words, dy_scales, a, w2, w1, gate, offs,
 
         def quantize_w1(grouped1, parts):
             count = grouped1.shape[1]
-            codes1 = work.tile([P, count, K], U32, name="codes1", align_bytes=64, bufs=5)
-            scales1 = work.tile([P, count, K], U8, name="scales1", align_bytes=64, bufs=5)
+            codes1 = work.tile([P, count, K], U32, name="codes1", align_bytes=64, bufs=len(W1_LOADS))
+            scales1 = work.tile([P, count, K], U8, name="scales1", align_bytes=64, bufs=len(W1_LOADS))
             for x in range(count):
                 for part in range(parts):
                     ks = slice(part * K // parts, (part + 1) * K // parts)
@@ -282,8 +281,8 @@ def tile_moe_bdx_mlp_relu_kernel(tc, dy_words, dy_scales, a, w2, w1, gate, offs,
         first_own = keep.tile([P, OWN_END - PLAIN_END], F32, name="first_own")
         first_closing = keep.tile([P, T - OWN_END], F32, name="first_closing")
         second_plain = keep.tile([P, PLAIN_END], F32, name="second_plain")
-        early = keep.tile([P, OWN_END], F32, name="early", align_bytes=SMALL_ALIGN)
-        late = keep.tile([P, T - OWN_END], F32, name="late", align_bytes=SMALL_ALIGN)
+        early = keep.tile([P, OWN_END], F32, name="early", align_bytes=DMA_ALIGN)
+        late = keep.tile([P, T - OWN_END], F32, name="late", align_bytes=DMA_ALIGN)
         nc.scalar.activation(out=first_plain[:], in_=fetched(pos1_sb, plain), func=COPY)
         nc.scalar.activation(out=first_closing[:], in_=fetched(pos1_sb, closing), func=COPY)
         nc.vector.tensor_copy(first_own[:], fetched(pos1_sb, own))

@@ -160,6 +160,18 @@ def tile_moe_bdx_mlp_relu_kernel(tc, dy_words, dy_scales, a, w2, w1, gate, offs,
             cols = slice(e * C, (e + 1) * C)
             nc.vector.quantize_mx(out=da_codes[:, cols].bitcast(FP8X4), scales=da_scales[:, cols], in_=da)
 
+        def warm_up(bank, codes, scales):
+            unread = psum.tile([P, HALF * C], F32, name="gate_bank", bufs=2)
+            nc.tensor.matmul_mx(
+                out=unread[:],
+                lhsT=codes.bitcast(FP8X4),
+                lhsT_scale=scales,
+                rhs=da_codes[:, :HALF * C].bitcast(FP8X4),
+                rhs_scale=da_scales[:, :HALF * C],
+                start=True,
+                stop=True,
+            )
+
         def load_w1(first, count):
             if first == E - 1:
                 raw1 = keep.tile([P, count, PACK, K], F32, name="dx", align_bytes=DMA_ALIGN)
@@ -251,12 +263,15 @@ def tile_moe_bdx_mlp_relu_kernel(tc, dy_words, dy_scales, a, w2, w1, gate, offs,
                 if e > 0 and o == 0:
                     da = raw[:, PACK - 1, SCALAR_M_FIRST * PACK:].bitcast(BF16)
                     make_da(e - 1, dh_before, da)
-                add_chunk(dh, e, o, *quantize_chunk(grouped, last))
+                codes, scales = quantize_chunk(grouped, last)
+                add_chunk(dh, e, o, codes, scales)
+                last_codes = (codes[:, PACK - 1, :], scales[:, PACK - 1, :])
                 if e > 0 and o == 0:
                     quantize_da(e - 1, da)
             if e == 0:
                 for pair in range(E // 2):
                     make_mask(pair)
+        warm_up(0, *last_codes)
         last_da = work.tile([P, C * PACK], BF16, name="last_da", align_bytes=64, bufs=1)
         make_da(E - 1, dh, last_da[:])
         quantize_da(E - 1, last_da[:])
@@ -272,6 +287,8 @@ def tile_moe_bdx_mlp_relu_kernel(tc, dy_words, dy_scales, a, w2, w1, gate, offs,
         dx = keep.tile([P, SLOTS], F32, name="dx", align_bytes=DMA_ALIGN)
         for group in ((0, 1, 2, 3), (4,), (5, 6), (7,)):
             make_dx(group[0], [coded_w1[e] for e in group], group[0] == 5)
+            if group[0] == 4:
+                warm_up(1, *coded_w1[4])
 
         def fetched(pos_sb, tokens):
             return dx[:].indirect(pos_sb[:, tokens.start // LIST_ROWS:tokens.stop // LIST_ROWS])

@@ -160,14 +160,14 @@ def tile_moe_bdx_mlp_relu_kernel(tc, dy_words, dy_scales, a, w2, w1, gate, offs,
             cols = slice(e * C, (e + 1) * C)
             nc.vector.quantize_mx(out=da_codes[:, cols].bitcast(FP8X4), scales=da_scales[:, cols], in_=da)
 
-        def warm_up(bank, codes, scales):
+        def warm_up(width, codes, scales):
             unread = psum.tile([P, HALF * C], F32, name="gate_bank", bufs=2)
             nc.tensor.matmul_mx(
-                out=unread[:],
+                out=unread[:, :width],
                 lhsT=codes.bitcast(FP8X4),
                 lhsT_scale=scales,
-                rhs=da_codes[:, :HALF * C].bitcast(FP8X4),
-                rhs_scale=da_scales[:, :HALF * C],
+                rhs=da_codes[:, :width].bitcast(FP8X4),
+                rhs_scale=da_scales[:, :width],
                 start=True,
                 stop=True,
             )
@@ -271,7 +271,8 @@ def tile_moe_bdx_mlp_relu_kernel(tc, dy_words, dy_scales, a, w2, w1, gate, offs,
             if e == 0:
                 for pair in range(E // 2):
                     make_mask(pair)
-        warm_up(0, *last_codes)
+        warm_up(512, *last_codes)
+        warm_up(256, *last_codes)
         last_da = work.tile([P, C * PACK], BF16, name="last_da", align_bytes=64, bufs=1)
         make_da(E - 1, dh, last_da[:])
         quantize_da(E - 1, last_da[:])
@@ -287,8 +288,8 @@ def tile_moe_bdx_mlp_relu_kernel(tc, dy_words, dy_scales, a, w2, w1, gate, offs,
         dx = keep.tile([P, SLOTS], F32, name="dx", align_bytes=DMA_ALIGN)
         for group in ((0, 1, 2, 3), (4,), (5, 6), (7,)):
             make_dx(group[0], [coded_w1[e] for e in group], group[0] == 5)
-            if group[0] == 4:
-                warm_up(1, *coded_w1[4])
+            if group[0] == 0:
+                warm_up(256, *coded_w1[3])
 
         def fetched(pos_sb, tokens):
             return dx[:].indirect(pos_sb[:, tokens.start // LIST_ROWS:tokens.stop // LIST_ROWS])

@@ -33,7 +33,8 @@ W2_LOADS = (1, 1, 1, 3, 3, 3, 3, 2, 2, 1, 1, 1, 1, 1)
 SCALAR_M_FIRST = 64
 SCALAR_M = 76
 SCALAR_M_LAST = 104
-W1_VECTOR_K = (0, K, 0, 0, 64, K, 0, 64)
+W1_VECTOR_K = (0, K, 0, 0, 0, 0, 64, 64)
+GPSIMD_EXPERT = 3
 W1_LOADS = ((0, 2), (2, 2), (4, 1), (5, 1), (6, 1), (7, 1))
 PLAIN_END = 160
 OWN_END = 320
@@ -183,6 +184,9 @@ def tile_moe_bdx_mlp_relu_kernel(tc, dy_words, dy_scales, a, w2, w1, gate, offs,
         def round_w1(raw, first, count):
             grouped1 = work.tile([P, count, K, PACK], BF16, name="grouped1", align_bytes=64, bufs=len(W1_LOADS))
             for x in range(count):
+                if first + x == GPSIMD_EXPERT:
+                    nc.gpsimd.tensor_copy(out=grouped1[:, x], in_=raw[:, x].rearrange("p t k -> p k t"))
+                    continue
                 dst = grouped1[:, x].rearrange("p (c i) t -> p c t i", i=4)
                 src = raw[:, x].rearrange("p t (c i) -> p c t i", i=4)
                 split = W1_VECTOR_K[first + x] // 4
@@ -286,8 +290,8 @@ def tile_moe_bdx_mlp_relu_kernel(tc, dy_words, dy_scales, a, w2, w1, gate, offs,
             for x, pair in enumerate(quantize_w1(piece, 2 if first == E - 1 else 1)):
                 coded_w1[first + x] = pair
         dx = keep.tile([P, SLOTS], F32, name="dx", align_bytes=DMA_ALIGN)
-        for group in ((0, 1, 2, 3), (4,), (5, 6), (7,)):
-            make_dx(group[0], [coded_w1[e] for e in group], group[0] == 5)
+        for group in ((0, 1, 2, 3), (4, 5, 6), (7,)):
+            make_dx(group[0], [coded_w1[e] for e in group], group[0] == 4)
             if group[0] == 0:
                 warm_up(256, *coded_w1[3])
 

@@ -161,18 +161,6 @@ def tile_moe_bdx_mlp_relu_kernel(tc, dy_words, dy_scales, a, w2, w1, gate, offs,
             cols = slice(e * C, (e + 1) * C)
             nc.vector.quantize_mx(out=da_codes[:, cols].bitcast(FP8X4), scales=da_scales[:, cols], in_=da)
 
-        def warm_up(width, codes, scales):
-            unread = psum.tile([P, HALF * C], F32, name="gate_bank", bufs=2)
-            nc.tensor.matmul_mx(
-                out=unread[:, :width],
-                lhsT=codes.bitcast(FP8X4),
-                lhsT_scale=scales,
-                rhs=da_codes[:, :width].bitcast(FP8X4),
-                rhs_scale=da_scales[:, :width],
-                start=True,
-                stop=True,
-            )
-
         def load_w1(first, count):
             if first == E - 1:
                 raw1 = keep.tile([P, count, PACK, K], F32, name="dx", align_bytes=DMA_ALIGN)
@@ -269,14 +257,11 @@ def tile_moe_bdx_mlp_relu_kernel(tc, dy_words, dy_scales, a, w2, w1, gate, offs,
                     make_da(e - 1, dh_before, da)
                 codes, scales = quantize_chunk(grouped, last)
                 add_chunk(dh, e, o, codes, scales)
-                last_codes = (codes[:, PACK - 1, :], scales[:, PACK - 1, :])
                 if e > 0 and o == 0:
                     quantize_da(e - 1, da)
             if e == 0:
                 for pair in range(E // 2):
                     make_mask(pair)
-        warm_up(512, *last_codes)
-        warm_up(256, *last_codes)
         last_da = work.tile([P, C * PACK], BF16, name="last_da", align_bytes=64, bufs=1)
         make_da(E - 1, dh, last_da[:])
         quantize_da(E - 1, last_da[:])
@@ -292,8 +277,6 @@ def tile_moe_bdx_mlp_relu_kernel(tc, dy_words, dy_scales, a, w2, w1, gate, offs,
         dx = keep.tile([P, SLOTS], F32, name="dx", align_bytes=DMA_ALIGN)
         for group in ((0, 1, 2, 3), (4, 5, 6), (7,)):
             make_dx(group[0], [coded_w1[e] for e in group], group[0] == 4)
-            if group[0] == 0:
-                warm_up(256, *coded_w1[3])
 
         def fetched(pos_sb, tokens):
             return dx[:].indirect(pos_sb[:, tokens.start // LIST_ROWS:tokens.stop // LIST_ROWS])

from contextlib import ExitStack

import concourse.mybir as mybir
from concourse.masks import make_identity

K, T, E, C, H, N = 128, 512, 8, 128, 512, 1536
SLOTS = E * C
FLOPS = 2 * SLOTS * (N * H + H * K)

F32 = mybir.dt.float32
BF16 = mybir.dt.bfloat16
I32 = mybir.dt.int32
U32 = mybir.dt.uint32
U16 = mybir.dt.uint16
U8 = mybir.dt.uint8
FP8X4 = mybir.dt.float8_e4m3fn_x4
ALU = mybir.AluOpType
COPY = mybir.ActivationFunctionType.Copy

P = 128
PACK = 4
K_PASS = P * PACK
PASSES = N // K_PASS
CHUNKS = E * PASSES
LIST_ROWS = 16
PAIR = 2 * C
HALF = E // 2
CHUNK_BYTES = PACK * H * 4
W1_BYTES = PACK * K * 4
PLACES = 12
DMA_ALIGN = 256
W2_LOADS = (1, 1, 1, 3, 3, 3, 3, 2, 2, 1, 1, 1, 1, 1)
SCALAR_M_FIRST = 64
SCALAR_M = 76
SCALAR_M_LAST = 104
W1_VECTOR_K = (0, K, 0, 0, 0, 0, 64, 64)
GPSIMD_EXPERT = 3
W1_LOADS = ((0, 2), (2, 2), (4, 1), (5, 1), (6, 1), (7, 1))
PLAIN_END = 160
OWN_END = 320


def tile_moe_bdx_mlp_relu_kernel(tc, dy_words, dy_scales, a, w2, w1, gate, offs, pos1, pos2, out):
    nc = tc.nc
    with ExitStack() as ctx:
        keep = ctx.enter_context(tc.tile_pool(name="keep", bufs=1))
        ring = ctx.enter_context(tc.tile_pool(name="ring", bufs=1))
        work = ctx.enter_context(tc.tile_pool(name="work", bufs=4))
        psum = ctx.enter_context(tc.psum_pool(name="psum", bufs=3))

        offs_sb = keep.tile([P, SLOTS // LIST_ROWS], U16, name="offs_sb", align_bytes=DMA_ALIGN)
        pos1_sb = keep.tile([P, T // LIST_ROWS], U16, name="pos1_sb", align_bytes=DMA_ALIGN)
        pos2_sb = keep.tile([P, T // LIST_ROWS], U16, name="pos2_sb", align_bytes=DMA_ALIGN)
        dy_w = keep.tile([P, PASSES, T], I32, name="dy_w", align_bytes=DMA_ALIGN)
        dy_s = keep.tile([P, T // 4], I32, name="dy_s", align_bytes=DMA_ALIGN)
        g_words = keep.tile([P, PASSES, SLOTS], U32, name="g_words", align_bytes=64)
        g_scales = keep.tile([P, SLOTS], U8, name="g_scales", align_bytes=64)
        gate_rows = keep.tile([P, C], F32, name="gate_rows", align_bytes=DMA_ALIGN)
        gate_cols = keep.tile([P, E], F32, name="gate_cols")
        identity = keep.tile([P, P], F32, name="identity")
        gate_banks = [psum.tile([P, HALF * C], F32, name="gate_bank", bufs=2) for half in range(2)]
        a_raw = keep.tile([P, PACK, SLOTS], F32, name="a_raw", align_bytes=DMA_ALIGN)
        gated_mask = keep.tile([P, SLOTS, PACK], F32, name="gated_mask")
        da_codes = keep.tile([P, SLOTS], U32, name="da_codes", align_bytes=64)
        da_scales = keep.tile([P, SLOTS], U8, name="da_scales", align_bytes=64)

        w2_chunks = w2.rearrange("e (o p j) i -> p (e o) j i", p=P, j=PACK)
        raws = []

        def load_chunks(count):
            first = len(raws)
            raw = ring.tile(
                [P, count, PACK, H], F32, name="raw%d" % first, align_bytes=DMA_ALIGN, offset=(first % PLACES) * CHUNK_BYTES
            )
            nc.sync.dma_start(out=raw[:], in_=w2_chunks[:, first:first + count])
            raws.extend(raw[:, x] for x in range(count))

        def round_chunk(raw, split, by_tile, first):
            grouped = work.tile([P, PACK, P, PACK], BF16, name="grouped", align_bytes=64)
            src = raw.rearrange("p j (m t) -> p m j t", t=PACK)
            dst = grouped[:].rearrange("p t m j -> p m j t")
            if by_tile:
                nc.scalar.copy(out=dst[:, :split, :, 2:], in_=src[:, :split, :, 2:])
                nc.vector.tensor_copy(out=dst[:, :, :, :2], in_=src[:, :, :, :2])
                nc.vector.tensor_copy(out=dst[:, split:, :, 2:], in_=src[:, split:, :, 2:])
            elif first:
                nc.scalar.activation(out=dst, in_=src, func=COPY)
            else:
                nc.scalar.copy(out=dst[:, :split], in_=src[:, :split])
                if split < P:
                    nc.vector.tensor_copy(out=dst[:, split:], in_=src[:, split:])
            return grouped

        def quantize_chunk(grouped, by_tile):
            codes = work.tile([P, PACK, P], U32, name="codes", align_bytes=64)
            scales = work.tile([P, PACK, P], U8, name="scales", align_bytes=64)
            for tiles in (slice(0, 2), slice(2, 4)) if by_tile else (slice(0, PACK),):
                nc.vector.quantize_mx(
                    out=codes[:, tiles, :].rearrange("p t m -> p (t m)").bitcast(FP8X4),
                    scales=scales[:, tiles, :].rearrange("p t m -> p (t m)"),
                    in_=grouped[:, tiles].rearrange("p t m j -> p (t m j)"),
                )
            return codes, scales

        def add_chunk(dh, e, o, codes, scales):
            cols = slice(e * C, (e + 1) * C)
            for t in range(PACK):
                nc.tensor.matmul_mx(
                    out=dh[:, t, :],
                    lhsT=codes[:, t, :].bitcast(FP8X4),
                    lhsT_scale=scales[:, t, :],
                    rhs=g_words[:, o, cols].bitcast(FP8X4),
                    rhs_scale=g_scales[4 * o:P, cols],
                    start=(o == 0 and t == 0),
                    stop=(o == PASSES - 1 and t == PACK - 1),
                )

        def gather_pair(pair, words):
            cols = slice(pair * PAIR, (pair + 1) * PAIR)
            entries = offs_sb[:, pair * PAIR // LIST_ROWS:(pair + 1) * PAIR // LIST_ROWS]
            if words:
                for o in range(PASSES):
                    nc.vector.tensor_copy(g_words[:, o, cols], dy_w[:, o, :].bitcast(U32).indirect(entries))
            else:
                nc.vector.tensor_copy(g_scales[:, cols], dy_s[:].bitcast(U8).indirect(entries))

        def spread_gate():
            nc.sync.dma_start(out=gate_rows[0:E, :], in_=gate[0:1, :].rearrange("r (e s) -> (r e) s", e=E))
            make_identity(nc, identity[:])
            turned = psum.tile([P, P], F32, name="acc")
            nc.tensor.transpose(turned[:], gate_rows[:], identity[:])
            nc.vector.tensor_copy(out=gate_cols[:], in_=turned[:, 0:E])
            for e in range(E):
                nc.tensor.transpose(
                    gate_banks[e // HALF][:, (e % HALF) * C:(e % HALF + 1) * C],
                    gate_cols[:, e:e + 1].to_broadcast([P, P]),
                    identity[:],
                )

        def make_mask(pair):
            cols = slice(pair * PAIR, (pair + 1) * PAIR)
            local = slice((pair % 2) * PAIR, (pair % 2 + 1) * PAIR)
            nc.vector.scalar_tensor_tensor(
                out=gated_mask[:, cols, :],
                in0=a_raw[:, :, cols].rearrange("p t s -> p s t"),
                scalar=0.0,
                in1=gate_banks[pair // 2][:, local].unsqueeze(2).to_broadcast([P, PAIR, PACK]),
                op0=ALU.is_gt,
                op1=ALU.mult,
            )

        def make_da(e, dh, da):
            nc.vector.tensor_tensor(
                out=da.rearrange("p (s t) -> p s t", t=PACK),
                in0=dh[:].rearrange("p t s -> p s t"),
                in1=gated_mask[:, e * C:(e + 1) * C, :],
                op=ALU.mult,
            )

        def quantize_da(e, da):
            cols = slice(e * C, (e + 1) * C)
            nc.vector.quantize_mx(out=da_codes[:, cols].bitcast(FP8X4), scales=da_scales[:, cols], in_=da)

        def load_w1(first, count):
            if first == E - 1:
                raw1 = keep.tile([P, count, PACK, K], F32, name="dx", align_bytes=DMA_ALIGN)
            else:
                raw1 = ring.tile([P, count, PACK, K], F32, name="raw1_%d" % first, align_bytes=DMA_ALIGN, offset=first * W1_BYTES)
            nc.sync.dma_start(out=raw1[:], in_=w1[first:first + count].rearrange("e (p t) k -> p e t k", t=PACK))
            return raw1

        def round_w1(raw, first, count):
            grouped1 = work.tile([P, count, K, PACK], BF16, name="grouped1", align_bytes=64, bufs=len(W1_LOADS))
            for x in range(count):
                if first + x == GPSIMD_EXPERT:
                    nc.gpsimd.tensor_copy(out=grouped1[:, x], in_=raw[:, x].rearrange("p t k -> p k t"))
                    continue
                dst = grouped1[:, x].rearrange("p (c i) t -> p c t i", i=4)
                src = raw[:, x].rearrange("p t (c i) -> p c t i", i=4)
                split = W1_VECTOR_K[first + x] // 4
                if split > 0:
                    nc.vector.tensor_copy(out=dst[:, :split], in_=src[:, :split])
                if split < K // 4:
                    nc.scalar.copy(out=dst[:, split:], in_=src[:, split:])
            return grouped1

        def quantize_w1(grouped1, parts):
            count = grouped1.shape[1]
            codes1 = work.tile([P, count, K], U32, name="codes1", align_bytes=64, bufs=len(W1_LOADS))
            scales1 = work.tile([P, count, K], U8, name="scales1", align_bytes=64, bufs=len(W1_LOADS))
            for x in range(count):
                for part in range(parts):
                    ks = slice(part * K // parts, (part + 1) * K // parts)
                    nc.vector.quantize_mx(
                        out=codes1[:, x, ks].bitcast(FP8X4),
                        scales=scales1[:, x, ks],
                        in_=grouped1[:, x, ks].rearrange("p k t -> p (k t)"),
                    )
            return [(codes1[:, x, :], scales1[:, x, :]) for x in range(count)]

        def make_dx(first, quantized, on_vector):
            count = len(quantized)
            acc = psum.tile([P, count * C], F32, name="dh" if on_vector else "acc")
            for x, (codes1, scales1) in enumerate(quantized):
                cols = slice((first + x) * C, (first + x + 1) * C)
                nc.tensor.matmul_mx(
                    out=acc[:, x * C:(x + 1) * C],
                    lhsT=codes1.bitcast(FP8X4),
                    lhsT_scale=scales1,
                    rhs=da_codes[:, cols].bitcast(FP8X4),
                    rhs_scale=da_scales[:, cols],
                    start=True,
                    stop=True,
                )
            if on_vector:
                nc.vector.tensor_copy(out=dx[:, first * C:(first + count) * C], in_=acc[:])
            else:
                nc.scalar.copy(out=dx[:, first * C:(first + count) * C], in_=acc[:])

        nc.gpsimd.memset(dy_s[:], 0)
        nc.gpsimd.memset(gate_rows[:], 0.0)
        nc.sync.dma_start(out=dy_w[:], in_=dy_words.rearrange("o p t d -> p o (t d)").bitcast(I32))
        nc.sync.dma_start(offs_sb[:], offs)
        load_chunks(W2_LOADS[0])
        for q in range(4):
            live = slice(32 * q, 32 * q + 4 * PASSES)
            nc.scalar.dma_start(out=dy_s[live, :], in_=dy_scales[:, 4 * q:4 * q + 4, :].bitcast(I32))
        load_chunks(W2_LOADS[1])
        load_chunks(W2_LOADS[2])
        for pair in range(E // 2):
            gather_pair(pair, True)
        for pair in range(E // 2):
            gather_pair(pair, False)
        spread_gate()
        nc.sync.dma_start(out=a_raw[:], in_=a.rearrange("(p t) s -> p t s", t=PACK))

        later_loads = list(W2_LOADS[3:])
        dh = None
        for e in range(E):
            dh_before = dh
            dh = psum.tile([P, PACK, C], F32, name="dh")
            for o in range(PASSES):
                c = e * PASSES + o
                if c == len(raws):
                    load_chunks(later_loads.pop(0))
                raw = raws[c]
                last = c == CHUNKS - 1
                if e == 0:
                    split = P
                elif o == 0:
                    split = SCALAR_M_FIRST
                else:
                    split = SCALAR_M_LAST if last else SCALAR_M
                grouped = round_chunk(raw, split, last, c == 0)
                if e > 0 and o == 0:
                    da = raw[:, PACK - 1, SCALAR_M_FIRST * PACK:].bitcast(BF16)
                    make_da(e - 1, dh_before, da)
                codes, scales = quantize_chunk(grouped, last)
                add_chunk(dh, e, o, codes, scales)
                if e > 0 and o == 0:
                    quantize_da(e - 1, da)
            if e == 0:
                for pair in range(E // 2):
                    make_mask(pair)
        last_da = work.tile([P, C * PACK], BF16, name="last_da", align_bytes=64, bufs=1)
        make_da(E - 1, dh, last_da[:])
        quantize_da(E - 1, last_da[:])

        w1_raw = [load_w1(first, count) for first, count in W1_LOADS]
        nc.sync.dma_start(pos1_sb[:], pos1)
        nc.sync.dma_start(pos2_sb[:], pos2)
        rounded = [round_w1(raw1, first, count) for (first, count), raw1 in zip(W1_LOADS, w1_raw)]
        coded_w1 = {}
        for (first, count), piece in zip(W1_LOADS, rounded):
            for x, pair in enumerate(quantize_w1(piece, 2 if first == E - 1 else 1)):
                coded_w1[first + x] = pair
        dx = keep.tile([P, SLOTS], F32, name="dx", align_bytes=DMA_ALIGN)
        for group in ((0, 1, 2, 3), (4, 5, 6), (7,)):
            make_dx(group[0], [coded_w1[e] for e in group], group[0] == 4)

        def fetched(pos_sb, tokens):
            return dx[:].indirect(pos_sb[:, tokens.start // LIST_ROWS:tokens.stop // LIST_ROWS])

        plain, own, closing = slice(0, PLAIN_END), slice(PLAIN_END, OWN_END), slice(OWN_END, T)
        first_plain = keep.tile([P, PLAIN_END], F32, name="first_plain")
        first_own = keep.tile([P, OWN_END - PLAIN_END], F32, name="first_own")
        first_closing = keep.tile([P, T - OWN_END], F32, name="first_closing")
        second_plain = keep.tile([P, PLAIN_END], F32, name="second_plain")
        early = keep.tile([P, OWN_END], F32, name="early", align_bytes=DMA_ALIGN)
        late = keep.tile([P, T - OWN_END], F32, name="late", align_bytes=DMA_ALIGN)
        nc.scalar.activation(out=first_plain[:], in_=fetched(pos1_sb, plain), func=COPY)
        nc.scalar.activation(out=first_closing[:], in_=fetched(pos1_sb, closing), func=COPY)
        nc.vector.tensor_copy(first_own[:], fetched(pos1_sb, own))
        nc.vector.tensor_copy(second_plain[:], fetched(pos2_sb, plain))
        nc.vector.tensor_tensor(early[:, own], fetched(pos2_sb, own), first_own[:], ALU.add)
        nc.vector.tensor_tensor(early[:, plain], second_plain[:], first_plain[:], ALU.add)
        nc.sync.dma_start(out=out[:, :OWN_END], in_=early[:])
        nc.vector.tensor_tensor(late[:], fetched(pos2_sb, closing), first_closing[:], ALU.add)
        nc.sync.dma_start(out=out[:, closing], in_=late[:])
